import numpy as np, ml_dtypes
CORES = [16,17,18,19,32,33,34,35]
N = 8
BF = ml_dtypes.bfloat16
def gentries(a):
    return np.ascontiguousarray(a.reshape(8, 16, -1).transpose(0, 2, 1)).reshape(8, -1)
def gtable(e):
    e = np.asarray(e); return np.ascontiguousarray(e.reshape(8, -1, 16).transpose(0, 2, 1)).reshape(128, -1).astype(np.int32)
V, RO, SH = 512, 3, 1
W = N * V
E = 16 * W
def join(ro, a, b):
    ro[a] = b; ro[b] = a
def couple(rng, ro, q):
    q = rng.permutation(q); h = len(q) // 2
    join(ro, q[:h], q[h:2 * h])
    if len(q) > 2 * h: ro[q[-1]] = q[-1]
def rest(rng, ro):
    couple(rng, ro, np.flatnonzero(ro < 0))
def pack(ro, X):
    x = np.ascontiguousarray(X.reshape(8, N, V, 16).transpose(1, 0, 3, 2)).reshape(N, 128, V)
    return {"rot": np.stack([gtable(ro[:, 16 * V * r:16 * V * (r + 1)]) for r in range(N)]), "x": x.astype(np.float32).astype(BF)}
def parities(rng, mode):
    par = np.zeros((8, N, V), np.int64)
    for r in range(N):
        c = int(mode[r])
        if c == 4: par[:, r] = rng.integers(0, 2, (8, V))
        if c in (1, 2): par[:, r] = 1
        if c in (2, 3): par[int(rng.integers(0, 8)), r, int(rng.integers(0, V))] ^= 1
    return par.reshape(8, W)
def voted(rng, ro, h, par, one):
    s = np.argsort(rng.random((W, 8)), axis=1)[:, :2]
    if one: s = np.full((W, 1), int(rng.integers(0, 8)))
    c = np.zeros((W, 16), bool); np.put_along_axis(c, 2 * s + par[:, None], True, 1); c = c.reshape(-1)
    free = ro < 0; hh = np.repeat(h, 16)
    join(ro, rng.permutation(np.flatnonzero(free & c & hh)), rng.permutation(np.flatnonzero(free & c & ~hh)))
    couple(rng, ro, np.flatnonzero(free & ~c & hh)); couple(rng, ro, np.flatnonzero(free & ~c & ~hh))
def nearly(rng, ro, X):
    q = np.concatenate([np.array([W - 1, 0]), 1 + rng.permutation(W - 2)[:10]])
    for b in range(4):
        i, j = sorted(int(v) for v in rng.permutation(16)[:2])
        if b & 1: i, j = j, i
        w, u, z = int(q[b]), int(q[4 + 2 * b]), int(q[5 + 2 * b]); e = 255 * int(rng.integers(0, 2))
        X[w] = e; X[u] = 255 - e; X[z] = 255 - e; X[u, int(rng.integers(0, 16))] = abs(254 - e)
        join(ro, 16 * w + i, 16 * u + int(rng.integers(0, 16))); join(ro, 16 * w + j, 16 * z + int(rng.integers(0, 16)))
def setup_inputs(rng):
    ro = np.full((8, E), -1, np.int64); X = rng.integers(0, 256, (8, W, 16))
    s = rng.integers(0, 32, (8, 8, 16)); pal = np.where(rng.random(s.shape) < 0.5, s, 255 - s)
    X = np.where(rng.random((8, W, 1)) < 0.25, pal[np.arange(8)[:, None], rng.integers(0, 8, (8, W))], X)
    for g in range(8):
        q = rng.permutation(E)[:32]; ro[g, q] = q
        rest(rng, ro[g])
    return pack(ro, X)
def setup_inputs_spread(rng):
    ro = np.full((8, E), -1, np.int64)
    X = np.minimum((np.exp2(9 * rng.random((8, W, 1)) - 2 * rng.random((8, 1, 16))) * rng.random((8, W, 16))).astype(np.int64), 255)
    share = rng.permutation(np.array([0.0, 0.1, 0.3, 0.5, 0.7, 0.8, 0.9, 0.97])); q = rng.permutation(N)
    for g in range(8):
        join(ro[g], 16 * V * int(q[0]) + rng.permutation(16 * V), 16 * V * int(q[1]) + rng.permutation(16 * V))
        for r in q[2:]:
            couple(rng, ro[g], 16 * V * int(r) + np.flatnonzero(rng.random(16 * V) < share[g]))
        rest(rng, ro[g])
    return pack(ro, X)
def setup_inputs_ends(rng):
    ro = np.full((8, E), -1, np.int64); mode = np.full(N, 4); mode[:3] = (0, 2, 3); mode[N - 1] = 1
    par = parities(rng, mode); X = np.zeros((8, W, 16), np.int64); z = 16 * (W - 1)
    for g in range(8):
        h = np.zeros(W, bool); h[rng.permutation(np.arange(1, W - 1))[:W // 2 - 1]] = True; h[W - 1] = True
        for i, j in (((15, 0), (1, 14), (8, 3)) if g % 2 == 1 else ((15, 0),)): join(ro[g], z + i, j)
        couple(rng, ro[g], z + np.flatnonzero(ro[g, z:] < 0)); couple(rng, ro[g], np.flatnonzero(ro[g, :16] < 0))
        voted(rng, ro[g], h, par[g], False)
        flip = np.zeros((W, 16), bool); np.put_along_axis(flip, rng.integers(0, 16, (W, 2)), True, 1)
        flip &= rng.random((W, 1)) < 0.75; flip[0] = False; flip[W - 1] = False
        X[g] = np.where(h[:, None] ^ flip, 255, 0)
    return pack(ro, X)
def setup_inputs_crowd(rng):
    ro = np.full((8, E), -1, np.int64); par = parities(rng, rng.permutation(N) & 3); X = np.zeros((8, W, 16), np.int64)
    for g in range(8):
        h = rng.permutation(W) < W // 2
        voted(rng, ro[g], h, par[g], g % 4 == 0)
        X[g] = rng.integers(0, 64, (W, 16)) + 192 * h[:, None]
    return pack(ro, X)
def setup_inputs_corners(rng):
    ro = np.full((8, E), -1, np.int64); a = np.arange(E); w = np.arange(W); kind = rng.permutation(8)
    for g in range(8):
        c = int(kind[g]); s = int(rng.integers(1, 16))
        if c == 0: ro[g] = a
        elif c == 1: ro[g] = a ^ s
        elif c == 2: ro[g] = E - 1 - a
        elif c == 3:
            for r in range(N): couple(rng, ro[g], 16 * V * r + np.arange(16 * V))
        elif c == 4: ro[g] = ((a + E // 2) % E) ^ s
        elif c == 5:
            step = (1, 2, 3, V, V - 1, W // 2, W - 1, 0)
            for b in range(8): join(ro[g], 16 * w + 2 * b, 16 * ((w + step[b]) % W) + 2 * b + 1)
        elif c == 6:
            q = rng.permutation(E)[:E // 2]; ro[g, q] = q; rest(rng, ro[g])
        else:
            join(ro[g], np.arange(16), E - 1 - np.arange(16)); rest(rng, ro[g])
    X = rng.integers(0, 256, (8, W, 16)); at = np.argsort(kind); o = at[rng.permutation(np.array([0, 1, 2, 4, 5]))]
    X[at[6]] = rng.integers(0, 256, 16)
    X[at[3]] = rng.integers(0, 255, 16) + rng.integers(0, 2, (W, 1))
    X[at[7]] = 255 * rng.integers(0, 2, (W, 1))
    X[o[0]] = 0; X[o[0], W - 1] = 255
    X[o[1]] = rng.integers(0, 2, (W, 16)); X[o[2]] = 255 - rng.integers(0, 3, (W, 16))
    return pack(ro, X)
def setup_inputs_ties(rng):
    ro = np.full((8, E), -1, np.int64); X = np.zeros((8, W, 16), np.int64)
    for g in range(8):
        b = rng.integers(64, 192, 16); d = rng.integers(1, 61, 16)
        X[g] = np.stack([b, b + d, b - d, b + rng.permutation(d)])[rng.integers(0, 4, W)]
        nearly(rng, ro[g], X[g])
        rest(rng, ro[g])
    return pack(ro, X)
def check_inputs(d):
    bad = []
    xf = np.asarray(d["x"]).astype(np.float64); r = np.asarray(d["rot"]).astype(np.int64)
    if not (np.min(xf) >= 0 and np.max(xf) <= 255): bad.append("range of x")
    if not np.array_equal(xf, np.floor(xf)): bad.append("whole numbers of x")
    if np.min(r) < 0 or np.max(r) > E - 1: bad.append("range of rot")
    full = np.clip(np.concatenate([gentries(a) for a in r], axis=1), 0, E - 1)
    if not np.array_equal(np.take_along_axis(full, full, 1), np.tile(np.arange(E), (8, 1))): bad.append("rot is its own inverse")
    return bad
def reference(rot, x):
    R = np.concatenate([gentries(a) for a in rot], axis=1).astype(np.int64)
    X = np.ascontiguousarray(x.astype(np.float32).astype(np.int32).reshape(N, 8, 16, V).transpose(1, 0, 3, 2)).reshape(8, W, 16)
    g = np.arange(8)[:, None]
    for t in range(RO):
        far = R >> 4
        Y = X[g, far].reshape(8, W, 16, 16)
        score = np.add.reduce(np.abs(Y - X[:, :, None, :]), axis=3)
        k = np.argmax(score, axis=2)
        A = np.add.reduce((k & 1).reshape(8, N, V), axis=(0, 2))
        m = (k + np.repeat(A, V)[None, :]) & 15; m = np.where(m == 0, 15, m)
        S = np.take_along_axis(R, 16 * far + ((R & 15) ^ m[g, far]), 1)
        X = ((2 ** SH - 1) * X + np.take_along_axis(Y, k[:, :, None, None], 2)[:, :, 0]) >> SH
        R = S
    yr = R.reshape(8, N, V, 16).transpose(1, 0, 3, 2).reshape(N, 128, V)
    yx = X.reshape(8, N, V, 16).transpose(1, 0, 3, 2).reshape(N, 128, V)
    return {"yr": np.ascontiguousarray(yr).astype(np.float32), "yx": np.ascontiguousarray(yx).astype(np.float32).astype(BF)}

@@ -1,0 +1,474 @@
+from concourse.bass import DstId, RemoteDMATransfer
+from concourse.mybir import AluOpType as OP, AxisListType as AX, ActivationFunctionType as AF
+
+RO = 3
+WN = 32768
+MAGIC = 12582912.0
+B, F, I, U = "bfloat16", "float32", "int32", "uint16"
+CFG = {
+    "ns": 8,
+    "fill": "vvvsvvssvvssssvv" "vvvvvssvvvsggggg",
+    "gm": "sssvsvsv",
+    "gr": "svssvssv",
+    "xr": "svvvsvvsvsssvvvs",
+    "offs": ((1, 3), (0, 1), (3, 4)),
+    "sel": ((1, 3), (0, 1), (3, 4)),
+    "bump": {},
+    "early": 12000.0, "ahead": 3, "xw": "vvsssvss", "xr0": "vvvvvvsvsvssvsvv",
+    "gm3": "ssvvssvs", "gr3": "vssvssss", "offs3": ((1, 3), (0, 1), (3, 4)),
+    "g": 1.5, "pe": 0.5, "dma": 1900.0, "rem": 2600.0, "link": 150.0, "delta": 120.0,
+}
+
+SCRATCH = {
+    "RW": ("sbuf", [128, WN], B), "XW": ("sbuf", [128, 4096], B), "MW": ("sbuf", [128, 4096], B),
+    "D": ("sbuf", [128, 8192], B), "G": ("sbuf", [128, 8192], B),
+    "XR": ("sbuf", [128, 8192], B), "RL": ("sbuf", [128, 8192], B),
+    "X": ("sbuf", [128, 512], B), "X2": ("sbuf", [128, 512], F), "XT": ("sbuf", [128, 512], B),
+    "SUM": ("sbuf", [128, 512], F), "SUM2": ("sbuf", [128, 512], F),
+    "ROT": ("sbuf", [128, 512], I), "R16": ("sbuf", [128, 512], U), "R16b": ("sbuf", [128, 512], U),
+    "RF": ("sbuf", [128, 512], F), "RI": ("sbuf", [128, 512], I), "FAR": ("sbuf", [128, 512], U),
+    "OFF": ("sbuf", [128, 512], U), "HI": ("sbuf", [128, 512], B), "LO": ("sbuf", [128, 512], B),
+    "SG": ("sbuf", [128, 512], F), "SJ": ("sbuf", [128, 512], I), "BS": ("sbuf", [128, 512], I),
+    "TA": ("sbuf", [128, 512], I), "TC": ("sbuf", [128, 512], I), "TF": ("sbuf", [128, 512], F),
+    "TD": ("sbuf", [128, 512], I), "TE": ("sbuf", [128, 512], I),
+    "SO": ("sbuf", [128, 512], F), "MB": ("sbuf", [128, 512], B),
+    "KI": ("sbuf", [128, 32], I), "KP": ("sbuf", [128, 32], I), "KK": ("sbuf", [128, 32], I),
+    "PB": ("sbuf", [128, 32], B), "KB": ("sbuf", [128, 32], B), "KT": ("sbuf", [128, 256], B),
+    "DL": ("sbuf", [128, 32], U), "ML": ("sbuf", [128, 32], U), "MI": ("sbuf", [128, 32], I), "MJ": ("sbuf", [128, 32], I),
+    "CNT": ("sbuf", [128, 16], F), "LAND": ("sbuf", [128, 24], F), "TOT": ("sbuf", [128, 4], F),
+    "IWv": ("sbuf", [128, 240], F), "IW": ("sbuf", [128, 240], B), "BOv": ("sbuf", [128, 128], F),
+    "BOc": ("sbuf", [128, 128], F), "BO": ("sbuf", [128, 128], B), "TB": ("sbuf", [128, 512], B),
+    "RM": ("sbuf", [128, 512], B), "C256": ("sbuf", [128, 32], B), "PI": ("sbuf", [128, 4], I), "PJ": ("sbuf", [128, 4], I),
+    "PW": ("sbuf", [128, 8], F), "SPi": ("sbuf", [128, 16], I), "SPj": ("sbuf", [128, 16], I), "SP": ("sbuf", [128, 16], B),
+    "GI": ("sbuf", [128, 8], F), "SEL": ("sbuf", [128, 1024], B), "EE": ("sbuf", [128, 2048], B), "WT": ("sbuf", [128, 6 * 144], B),
+    "SX": ("dram", [8, 128, 64], B), "LX": ("dram", [8, 128, 64], B),
+    "SR": ("dram", [8, 128, 64], U), "LR": ("dram", [8, 128, 64], U),
+    "SX2": ("dram", [8, 128, 64], B), "LX2": ("dram", [8, 128, 64], B),
+    "SO4": ("dram", [32, 128, 16], F), "LO4": ("dram", [32, 128, 16], F),
+    "DX": ("dram", [16, 8, 512], B), "DR": ("dram", [4, 16, 2048], B),
+}
+for _b in range(8):
+    SCRATCH["ps%d" % _b] = ("psum", [128, 512], F)
+
+SEMAPHORES = (["cv", "cs", "cp", "cg", "ax", "lx", "ar", "lr", "ax2", "lx2"]
+              + ["ae%d" % t for t in range(RO)] + ["le%d" % t for t in range(RO)]
+              + ["ao%d" % q for q in range(4)] + ["lo%d" % q for q in range(4)]
+              + ["d%d" % k for k in range(60)])
+
+
+def engine_plan(topo, cores, src):
+    off = [c for c in cores if topo.chip(c) != topo.chip(src)]
+    on = [c for c in cores if c != src and topo.chip(c) == topo.chip(src)]
+    eoff = topo.engines(src, off[0])
+    eon = [e for e in topo.engines(src, on[0]) if e not in eoff]
+    plan = {}
+    for dsts, eng in ((off, eoff), (on, eon)):
+        n = 1
+        while 2 * n * len(dsts) <= len(eng):
+            n *= 2
+        for k, c in enumerate(dsts):
+            plan[c] = eng[k * n:(k + 1) * n]
+    return plan
+
+
+def order(tasks):
+    n = len(tasks)
+    succ = [[] for _ in range(n)]
+    for k, t in enumerate(tasks):
+        for p, _w in t["pre"]:
+            succ[p].append(k)
+    level = [0.0] * n
+    for k in range(n - 1, -1, -1):
+        level[k] = tasks[k]["hold"] + tasks[k]["lat"] + tasks[k].get("early", 0.0) + max([level[s] for s in succ[k]], default=0.0)
+    for k, d in CFG["bump"].items():
+        level[k] += d
+    left = [len(set(p for p, _w in t["pre"])) for t in tasks]
+    succ = [sorted(set(s)) for s in succ]
+    est, free, out = {}, {}, []
+    fin, end = [0.0] * n, [0.0] * n
+    for k in range(n):
+        if left[k] == 0:
+            est[k] = 0.0
+    while est:
+        t0, q = min((max(e, free.get(tasks[k]["q"], 0.0)), tasks[k]["q"]) for k, e in est.items())
+        k = max((level[k], -k) for k, e in est.items() if tasks[k]["q"] == q and e <= t0 + CFG["delta"])
+        k = -k[1]
+        st = max(est.pop(k), free.get(q, 0.0))
+        end[k] = free[q] = st + tasks[k]["hold"]
+        fin[k] = end[k] + tasks[k]["lat"]
+        out.append(k)
+        tasks[k]["at"] = st
+        for s in succ[k]:
+            left[s] -= 1
+            if left[s] == 0:
+                est[s] = max(fin[p] if w else end[p] for p, w in tasks[s]["pre"])
+    CFG["span"] = max(fin)
+    return out
+
+
+def rank_program(g, core, T, topo):
+    me = T.rank_of(core)
+    if me is None:
+        return
+    cores = list(T.cores)
+    NS, GC = CFG["ns"], CFG["g"]
+    Q = {"v": g.vector, "s": g.scalar, "p": g.tensor, "y": g.sync, "g": g}
+    tasks, writer, readers, bank, base = [], {}, {}, {}, {}
+
+    def task(q, kind, body, hold, lat, R=(), W=(), P=(), acc=None):
+        k = len(tasks)
+        same = lambda p: kind == "op" and tasks[p]["kind"] == "op" and tasks[p]["q"] == q
+        pre = [(writer[x], "W") for x in R if x in writer]
+        for x in W:
+            if x in writer:
+                pre.append((writer[x], "W"))
+            pre += [(p, "R") for p in readers.get(x, [])]
+        for b in P:
+            if acc is not None and acc not in base:
+                base[acc] = list(bank.get(b, []))
+                bank[b] = []
+            pre += [(p, None if same(p) else "W") for p in (base[acc] if acc is not None else bank.get(b, []))]
+            bank[b] = (bank[b] if acc is not None else []) + [k]
+        tasks.append({"q": q, "kind": kind, "body": body, "hold": hold, "lat": lat, "pre": pre, "acc": acc,
+                      "name": (list(W) + list(P) + ["-"])[0]})
+        for x in R:
+            readers.setdefault(x, []).append(k)
+        for x in W:
+            writer[x] = k
+            readers[x] = []
+
+    def op(q, call, d, R=(), W=(), P=()):
+        task(q, "op", [call], max(d, 64) + (60 if d > 64 else 20), 100, R, W, P)
+
+    def dma(q, moves, kb, R=(), W=(), early=0.0):
+        task(q, "dma", moves, 60 * len(moves), CFG["dma"] + 4 * kb, R, W)
+        tasks[-1]["early"] = early
+
+    def exchange(src_of, dst_of, sa, sl, kb, R, W):
+        task("g", "rem", (src_of, dst_of, sa, sl), 600 + CFG["link"] * kb, CFG["rem"], R, W)
+
+    V, S, PE = g.vector, g.scalar, g.tensor
+    ps = [T["ps%d" % b] for b in range(8)]
+    ID = T.IW[:, 112:240]
+    blk = lambda n, a, b: [(n, c) for c in range(a, b)]
+    rng4 = lambda n: blk(n, 0, 4)
+
+    def ts(d, out, in0, a, b, o0, o1=None, R=(), W=(), P=()):
+        if o1 is None:
+            op("v", lambda: V.tensor_scalar(out, in0, a, None, o0), d, R, W, P)
+        else:
+            op("v", lambda: V.tensor_scalar(out, in0, a, b, o0, o1), d, R, W, P)
+
+    def tt(d, out, in0, in1, o, R=(), W=(), P=()):
+        op("v", lambda: V.tensor_tensor(out, in0, in1, o), d, R, W, P)
+
+    def cp(d, out, in_, R=(), W=(), P=()):
+        op("v", lambda: V.tensor_copy(out, in_), d, R, W, P)
+
+    def act(d, out, in_, fn, R=(), W=(), P=(), **kw):
+        op("s", lambda: S.activation(out, in_, fn, **kw), d, R, W, P)
+
+    def mms(b, n, lst, R, acc=None):
+        task("p", "op" if acc is None else "op", [(lambda a=a: PE.matmul(*a)) for a in lst] if acc is None else lst,
+             max(n, 64) * CFG["pe"] * len(lst), 160, R, (), (b,), acc)
+
+    def iota(d, out, pattern, base_, cm, W):
+        op("g", lambda: g.iota(out, pattern, base_, cm, allow_small_or_imprecise_dtypes=True), 2 * d + 80, (), W)
+
+    wt = lambda k, c: T.WT[:, 144 * k + 15 - c:144 * k + 143 - c]
+    W_RELU, W_NEG, W_ABS, W_M, W_SUM, W_DIF = range(6)
+
+    dma("y", [(T.SX[:], T.x[:])], 128, (), ["SX"])
+    dma("s", [(T.ROT[:], T.rot[:])], 256, (), ["ROT"])
+    dma("y", [(T.LX[me], T.x[16 * me:16 * me + 16, :])], 16, (), ["LXo"])
+    iota(240, T.IWv[:], [[1, 240]], -112, -1, ["IWv"])
+    iota(128, T.BOv[:], [[-16, 8], [0, 16]], 0, 1, ["BOv"])
+    op("g", lambda: g.iota(T.PI[:, 0:1], [[0, 1]], 0, 1), 100, (), ["PI"])
+    iota(32, T.C256[:], [[256, 32]], 0, 0, ["C256"])
+    iota(512, T.TB[:], [[0, 32], [-1, 16]], 15, 0, ["TB"])
+    exchange(lambda r: T.SX[r], lambda r: T.LX[me], "ax", "lx", 16, ["SX"], ["LX"])
+    cp(512, T.R16[:], T.ROT[:], ["ROT"], ["R16"])
+    dma("y", [(T.SR[:], T.R16[:])], 128, ["R16"], ["SR"])
+    dma("y", [(T.LR[me], T.R16[16 * me:16 * me + 16, :])], 16, ["R16"], ["LRo"])
+    exchange(lambda r: T.SR[r], lambda r: T.LR[me], "ar", "lr", 16, ["SR"], ["LR", "sent"])
+    k = 0
+    while k < 32:
+        q, n = CFG["fill"][k], 1
+        while q != "s" and k + n < 32 and CFG["fill"][k + n] == q and (q == "g" or n < 2):
+            n += 1
+        w = T.RW[:, 1024 * k:1024 * (k + n)]
+        if q == "v":
+            op("v", lambda w=w: V.memset(w, 0.0), 512 * n, (), blk("Z", k, k + n))
+        elif q == "s":
+            act(1024, w, T.RW[:, 0:1024], AF.Copy, [("Z", 0)], [("Z", k)])
+        else:
+            op("g", lambda w=w, n=n: g.iota(w, [[0, 1024 * n]], 0, 0, allow_small_or_imprecise_dtypes=True),
+               2048 * n, ["SR"], blk("Z", k, k + n))
+        k += n
+    op("g", lambda: g.iota(T.MW[:], [[0, 4096]], 0, 0, allow_small_or_imprecise_dtypes=True), 8192, ["SR"], ["MWv", "MWs"])
+
+    ts(240, T.IW[:], T.IWv[:], 0.0, None, OP.is_equal, None, ["IWv"], ["IW"])
+    ts(128, T.BOc[:], T.BOv[:], 0.0, 15.0, OP.max, OP.min, ["BOv"], ["BOc"])
+    op("v", lambda: V.memset(T.WT[:], 0.0), 432, (), ["WT0"])
+    ts(1, T.PJ[:, 0:1], T.PI[:, 0:1], 15, None, OP.bitwise_and, None, ["PI"], ["PJ"])
+    ts(256, T.RM[:], T.TB[:], 15.0, None, OP.not_equal, None, ["TB"], ["RM"])
+    tt(256, T.BO[:], T.BOc[:], T.BOv[:], OP.is_equal, ["BOc", "BOv"], ["BO"])
+    ts(16, T.SPi[:], T.TB[:, 0:16], -17.0, 255.0, OP.mult, OP.add, ["TB"], ["SPi"])
+    ts(1, T.PW[:, 0:1], T.PJ[:, 0:1], 16.0, None, OP.mult, None, ["PJ"], ["PW0"])
+    ts(1, T.PW[:, 1:2], T.PJ[:, 0:1], 0.0, None, OP.is_equal, None, ["PJ"], ["PW1"])
+    ts(1, T.PW[:, 2:3], T.PJ[:, 0:1], 4.0, 0.5, OP.is_lt, OP.mult, ["PJ"], ["PW2"])
+    ts(1, T.PW[:, 3:4], T.PJ[:, 0:1], 2.0, None, OP.is_lt, None, ["PJ"], ["PW3"])
+    op("v", lambda: V.memset(T.SPi[:, 0:1], 255), 1, ["SPi"], ["SPi"])
+    tt(1, T.PW[:, 4:5], T.PW[:, 2:3], T.PW[:, 3:4], OP.subtract, ["PW2", "PW3"], ["PW4"])
+    for k, w in enumerate((32.0, -16.0, 16.0, T.PW[:, 1:2], T.PW[:, 2:3], T.PW[:, 4:5])):
+        ts(8, T.WT[:, 144 * k + 15:144 * k + 143:16], T.BO[:, 0:128:16], w, None, OP.mult, None,
+           ["BO", "WT0", "PW1", "PW2", "PW4"], [("WT", k)])
+    ts(16, T.SPj[:], T.SPi[:], 165, None, OP.bitwise_and, None, ["SPi"], ["SPj"])
+    for i in range(16):
+        ts(64, T.EE[:, i:2048:16], ID, -1.0, None, OP.mult, None, ["IW"], [("EE", i)])
+    cp(16, T.SP[:], T.SPj[:], ["SPj"], ["SP"])
+
+    dma("y", [(T.X[:], T.LX[:])], 128, ["LX", "LXo"], ["X"])
+    dma("y", [(T.R16b[:], T.LR[:])], 128, ["LR", "LRo"], ["R16b"])
+    XWK = blk("XW", 0, 8)
+    ts(1, T.PW[:, 5:6], T.PJ[:, 0:1], -1.0, 15.0, OP.mult, OP.add, ["PJ"], ["PW5"])
+    cp(8, T.GI[:], T.BO[:, 0:128:16], ["BO"], ["GI"])
+    for r in range(8):
+        sel = T.SEL[:, 128 * r:128 * r + 128]
+        ts(64, sel, T.TB[:, 0:128], T.PW[:, 5:6], T.GI[:, r:r + 1], OP.is_equal, OP.mult,
+           ["TB", "PW5", "GI"], [("SEL", r)])
+        b, out = (0, 1, 2, 3, 4, 5, 7, 0)[r], T.XW[:, 512 * r:512 * r + 512]
+        mms(b, 512, [(ps[b][:], sel, T.X[:], True, True)], [("SEL", r), "X"])
+        if CFG["xw"][r] == "v":
+            cp(512, out, ps[b][:], (), [("XW", r)], (b,))
+        else:
+            act(512, out, ps[b][:], AF.Copy, (), [("XW", r)], (b,))
+
+    def x_window_load(after):
+        dma("y", [(T.XW[16 * r:16 * r + 16, :], T.DX[:]) for r in range(8)], 1024, ["DX"] + after, XWK)
+
+    v0 = 32 * NS
+
+    def x_forms(who):
+        act(512 - v0, T.X2[:, v0:512], T.X[:, v0:512], AF.Identity, ["X"], ["X2b"], scale=2.0)
+        nb = (NS + 3) // 4
+        mms(6, 128, [(ps[6][:, 128 * vb:128 * vb + 128], T.X[:, 128 * vb:128 * vb + 128], ID, True, True)
+                     for vb in range(nb)], ["X", "IW"])
+        act(128 * nb, T.XT[:, 0:128 * nb], ps[6][:, 0:128 * nb], AF.Copy, (), ["XT"], (6,))
+        for i in range(16):
+            out, in_ = T.XR[:, 16 * v0 + i:8192:16], T.X[:, v0:512]
+            if who[i] == "v":
+                cp((512 - v0) // 2, out, in_, ["X"], [("XR", i)])
+            else:
+                act(512 - v0, out, in_, AF.Copy, ["X"], [("XR", i)])
+
+    def lists_and_digits(qa, qb, src, sk):
+        a, b = 128 * qa, 128 * qb
+        ts(b - a, T.FAR[:, a:b], src[:, a:b], 0.0625, -0.46875, OP.mult, OP.add, sk, blk("FAR", qa, qb))
+        act(b - a, T.HI[:, a:b], T.RF[:, a:b], AF.Copy, blk("RF", qa, qb), blk("HI", qa, qb))
+        tt(2 * (b - a), T.LO[:, a:b], T.RF[:, a:b], T.HI[:, a:b], OP.subtract, blk("RF", qa, qb) + blk("HI", qa, qb),
+           blk("LO", qa, qb))
+
+    def r_window_load(h, after):
+        a, b = h * WN // 2, (h + 1) * WN // 2
+        dma("y", [(T.RW[16 * r:16 * r + 4, a:b], T.DR[:, 8 * h:8 * h + 8, :]) for r in range(8)], 1024, ["DR"] + after,
+            blk("Z", 16 * h, 16 * h + 16), CFG["early"] if h == 0 else 0.0)
+
+    def r_window_store():
+        dma("y", [(T.DR[2 * (r // 4) + d, :, 512 * (r % 4):512 * (r % 4) + 512], buf[16 * r:16 * r + 16, :])
+                  for d, buf in enumerate((T.HI, T.LO)) for r in range(8)], 256, rng4("HI") + rng4("LO"), ["DR"])
+        r_window_load(0, [])
+
+    x_forms(CFG["xr0"])
+    cp(512, T.RF[:], T.R16b[:], ["R16b"], rng4("RF"))
+    lists_and_digits(0, 4, T.R16b, ["R16b"])
+    r_window_store()
+
+    for t in range(RO):
+        last = t == RO - 1
+        XRK, EEK, acc = blk("XR", 0, 16), blk("EE", 0, 16), "key%d" % t
+        mms(0, 512, [(ps[0][:], ID, T.TB[:], True, False)], ["IW", "TB"])
+
+        def key(k, c, buf, name):
+            mms(0, 512, [(ps[0][:], wt(k, c), buf[:, 512 * c:512 * c + 512])], [(name, c), ("WT", k)], acc)
+
+        first = [q for qa, qb in CFG["sel"] for q in range(qa, qb)] if t > 0 else [0, 1, 2, 3]
+        done = []
+        for n, c in enumerate(sorted(range(NS), key=lambda c: (first.index(c // 4), c))):
+            b = 1 + n % 4
+            mms(b, 512, [(ps[b][:], T.XT[:, 128 * (c // 4):128 * (c // 4) + 128],
+                          T.EE[:, 512 * (c % 4):512 * (c % 4) + 512], True, False)], ["XT"] + EEK)
+            act(512 * GC, T.D[:, 512 * c:512 * c + 512], T.XW[:, :].indirect(T.FAR[:, 32 * c:32 * c + 32]), AF.Copy,
+                XWK + [("FAR", c // 4)], [("D", c)])
+            if n >= CFG["ahead"]:
+                tasks[-1]["pre"].append((done[n - CFG["ahead"]], None))
+            mms(b, 512, [(ps[b][:], ID, T.D[:, 512 * c:512 * c + 512], False, True)], ["IW", ("D", c)])
+            act(512, T.RL[:, 512 * c:512 * c + 512], ps[b][:], AF.Abs, (), [("RL", c)], (b,))
+            done.append(len(tasks) - 1)
+            key(W_ABS, c, T.RL, "RL")
+        a, done = NS, []
+        while a < 16:
+            b = a + 2 if a + 3 < 16 and a % 2 == 0 else a + 1
+            tt(512 * GC * (b - a), T.D[:, 512 * a:512 * b], T.XW[:, :].indirect(T.FAR[:, 32 * a:32 * b]),
+               T.XR[:, 512 * a:512 * b], OP.subtract, XWK + [("FAR", a // 4)] + XRK, blk("D", a, b))
+            if len(done) >= 2:
+                tasks[-1]["pre"].append((done[-2], None))
+            ts(256 * (b - a), T.RL[:, 512 * a:512 * b], T.D[:, 512 * a:512 * b], 0.0, None, OP.max, None,
+               blk("D", a, b), blk("RL", a, b))
+            done.append(len(tasks) - 1)
+            for c in range(a, b):
+                key(W_NEG, c, T.D, "D")
+                key(W_RELU, c, T.RL, "RL")
+            a = b
+
+        op("v", lambda: V.tensor_tensor_scan(T.SO[:], T.RM[:], ps[0][:], 0.0, OP.mult, OP.max), 512, ["RM"], ["SO"], (0,))
+        cp(32, T.KI[:], T.SO[:, 15:512:16], ["SO"], ["KI"])
+        ts(32, T.KP[:], T.KI[:], 1, None, OP.bitwise_and, None, ["KI"], ["KP"])
+        ts(32, T.KK[:], T.KI[:], 15, None, OP.bitwise_and, None, ["KI"], ["KK"])
+        cp(32, T.PB[:], T.KP[:], ["KP"], ["PB"])
+        ts(32, T.KB[:], T.KK[:], -1.0, 15.0, OP.mult, OP.add, ["KK"], ["KB"])
+        own = T.CNT[:, 4 * t:4 * t + 1]
+        mms(7, 32, [(ps[7][:, 0:32], T.BO[:], T.PB[:], True, True)], ["BO", "PB"])
+        op("v", lambda own=own: V.tensor_reduce(own, ps[7][:, 0:32], AX.X, OP.add), 32, (), [("CNT", t)], (7,))
+        slot = lambda r, t=t: 8 * t + (me if me < r else me - 1)
+        exchange(lambda r, own=own: own, lambda r, slot=slot: T.LAND[:, slot(r):slot(r) + 1], "ae%d" % t, "le%d" % t, 0,
+                 [("CNT", t)], [("LAND", t)])
+        mms(6, 128, [(ps[6][0:16, h:256:2], T.KB[:, 16 * h:16 * h + 16], ID, True, True) for h in range(2)], ["KB", "IW"])
+        act(256, T.KT[0:16, :], ps[6][0:16, 0:256], AF.Copy, (), ["KT"], (6,))
+        mms(1, 32, [(ps[1][:, 0:32], ID, T.C256[:], True, False)]
+            + [(ps[1][:, 0:32], T.IW[0:16, 112 - 16 * r:240 - 16 * r], T.KT[0:16, 32 * r:32 * r + 32], False, r == 7)
+               for r in range(8)], ["IW", "KT", "C256"])
+        ts(32, T.DL[:], ps[1][:, 0:32], T.PW[:, 0:1], None, OP.add, None, ["PW0"], ["DL"], (1,))
+        tt(v0 * GC, T.SUM[:, 0:v0], T.D[:, :].indirect(T.DL[:, 0:2 * NS]), T.X[:, 0:v0], OP.add,
+           blk("D", 0, 16) + ["DL", "X"], ["SUMa"])
+        tt((512 - v0) * GC, T.SUM[:, v0:512], T.D[:, :].indirect(T.DL[:, 2 * NS:32]), T.X2[:, v0:512], OP.add,
+           blk("D", 0, 16) + ["DL", "X2b"], ["SUMb"])
+        act(512, T.SUM2[:], T.SUM[:], AF.Identity, ["SUMa", "SUMb"], ["SUM2"], bias=MAGIC, scale=0.4995)
+        act(512, T.X[:], T.SUM2[:], AF.Identity, ["SUM2"], ["X"], bias=-MAGIC, scale=1.0)
+        act(512, T.SG[:], T.RF[:], AF.Sign, rng4("RF"), ["SG"], bias=-32767.5, scale=1.0)
+        cp(512, T.RI[:], T.RF[:], rng4("RF") + ["SO"], ["RI"])
+        ts(512, T.TD[:], T.RI[:], 15, None, OP.bitwise_and, None, ["RI"], ["TD"])
+        ts(512, T.TE[:], T.TD[:], 17.0, None, OP.mult, None, ["TD"], ["TE"])
+        ts(512, T.SJ[:], T.TE[:], 165, None, OP.bitwise_and, None, ["TE"], ["SJ"])
+        ts(512, T.BS[:], T.RI[:], 4, 2047, OP.logical_shift_right, OP.bitwise_and, ["RI"], ["BS"])
+        tot, land = T.TOT[:, 0:1], T.LAND[:, 8 * t:8 * t + 7]
+        op("v", lambda land=land: V.tensor_reduce(tot, land, AX.X, OP.add), 8, [("LAND", t)], ["TOT"])
+        ts(32, T.MI[:], ps[1][:, 0:32], tot, own, OP.subtract, OP.subtract, ["TOT", ("CNT", t)], ["MI"], (1,))
+        ts(32, T.MJ[:], T.MI[:], 15, None, OP.bitwise_and, None, ["MI"], ["MJ"])
+        cp(32, T.ML[:], T.MJ[:], ["MJ"], ["ML"])
+        cp(256 * GC, T.MB[:, 0:256], T.SP[:, :].indirect(T.ML[:, 0:16]), ["SP", "ML"], ["MB0"])
+        act(256 * GC, T.MB[:, 256:512], T.SP[:, :].indirect(T.ML[:, 16:32]), AF.Copy, ["SP", "ML"], ["MB1"])
+        for q, kk in (("y", "MWv"), ("s", "MWs")):
+            dma(q, [(T.MW[0:128:16, 512 * r:512 * r + 512], T.MB[16 * r:16 * r + 8, :])
+                    for r in range(8) if "ys"[r % 2] == q], 32, ["MB0", "MB1"], [kk, kk + "i"])
+        r_window_load(1, ["MWvi", "MWsi"])
+        if last:
+            dma("y", [(T.SX2[:], T.X[:])], 128, ["X", "MWvi"], ["SX2"])
+            dma("y", [(T.LX2[me], T.X[16 * me:16 * me + 16, :])], 16, ["X", "MWvi"], ["LX2o"])
+            exchange(lambda r: T.SX2[r], lambda r: T.LX2[me], "ax2", "lx2", 16, ["SX2"], ["LX2"])
+            dma("y", [(T.yx[:], T.LX2[:])], 128, ["LX2", "LX2o"], ["yx"])
+        else:
+            x_forms(CFG["xr"])
+            dma("y", [(T.DX[:, r, :], T.X[16 * r:16 * r + 16, :]) for r in range(8)], 128, ["X", "MWvi"], ["DX"])
+            x_window_load([("Z", 31)])
+
+        def gather(q, buf, name, win, wk, lst, lk, n):
+            out, src = buf[:, 1024 * n:1024 * n + 1024], win[:, :].indirect(lst[:, 64 * n:64 * n + 64])
+            R, W = wk + [(lk, n // 2)], blk(name, 2 * n, 2 * n + 2)
+            if q == "v":
+                cp(1024 * GC, out, src, R, W)
+            else:
+                act(1024 * GC, out, src, AF.Copy, R, W)
+
+        def collect(pb, c0, k, buf, name, h):
+            mms(pb, 64, [(ps[pb][:, c0:c0 + 64], wt(k, i), buf[:, 1024 * h + i:1024 * h + 1024:16], i == 0, i == 15)
+                         for i in range(16)], blk(name, 2 * h, 2 * h + 2) + [("WT", k)])
+
+        tag = "3" if last else ""
+        for n, (qa, qb) in enumerate(CFG["offs" + tag]):
+            pb, a, b = 3 + n % 2, 128 * qa, 128 * qb
+            for q in range(qa, qb):
+                for h in (2 * q, 2 * q + 1):
+                    gather(CFG["gm" + tag][h], T.D, "D", T.MW, ["MWv", "MWs"], T.FAR, "FAR", h)
+                    collect(pb, 64 * h - a, W_M, T.D, "D", h)
+            ta, tc, ka, kc = T.TA[:, a:b], T.TC[:, a:b], blk("TA", qa, qb), blk("TC", qa, qb)
+            tt(b - a, ta, ps[pb][:, 0:b - a], T.SJ[:, a:b], OP.add, ["SJ"], ka, (pb,))
+            ts(b - a, tc, ta, 165, None, OP.bitwise_and, None, ka, kc)
+            ts(b - a, ta, tc, 2176.0, None, OP.mult, None, kc, ka)
+            ts(b - a, tc, ta, 0x7800, None, OP.bitwise_and, None, ka, kc)
+            tt(2 * (b - a), ta, tc, T.BS[:, a:b], OP.add, kc + ["BS"], ka)
+            cp(b - a, T.OFF[:, a:b], ta, ka, blk("OFF", qa, qb))
+
+        one = [(q, q + 1) for qa, qb in CFG["offs" + tag] for q in range(qa, qb)]
+        for n, (qa, qb) in enumerate(one if last else CFG["sel"]):
+            pb, a, b = 5 + n % 3, 128 * qa, 128 * qb
+            for q in range(qa, qb):
+                for h in (2 * q, 2 * q + 1):
+                    gather(CFG["gr" + tag][h], T.G, "G", T.RW, blk("Z", 0, 32), T.OFF, "OFF", h)
+                    collect(pb, 256 + 64 * h - a, W_DIF, T.G, "G", h)
+                    collect(pb, 64 * h - a, W_SUM, T.G, "G", h)
+            tt(b - a, T.TF[:, a:b], ps[pb][:, 256:256 + b - a], T.SG[:, a:b], OP.mult, ["SG"], blk("TF", qa, qb), (pb,))
+            tt(b - a, T.RF[:, a:b], ps[pb][:, 0:b - a], T.TF[:, a:b], OP.add, blk("TF", qa, qb), blk("RF", qa, qb), (pb,))
+            if not last:
+                lists_and_digits(qa, qb, T.RF, blk("RF", qa, qb))
+                continue
+            q = qa
+            dma("y", [(T.SO4[8 * q:8 * q + 8], T.RF[:, a:b])], 64, [("RF", q)], [("SO4", q)])
+            dma("y", [(T.LO4[8 * q + me], T.RF[16 * me:16 * me + 16, a:b])], 8, [("RF", q)], [("LO4o", q)])
+            exchange(lambda r, q=q: T.SO4[8 * q + r], lambda r, q=q: T.LO4[8 * q + me], "ao%d" % q, "lo%d" % q, 8,
+                     [("SO4", q)], [("LO4", q)])
+        if not last:
+            r_window_store()
+    for q in range(4):
+        dma("s", [(T.yr[:, 128 * q:128 * q + 128], T.LO4[8 * q:8 * q + 8])], 64,
+            [("LO4", q), ("LO4o", q)] + blk("G", 0, 16), [("yr", q)])
+
+    plans = {c: engine_plan(topo, cores, c) for c in cores}
+    total, known, tok, nd, todo = {}, {q: {} for q in Q}, {}, [0], {}
+    for tk in tasks:
+        todo[tk["acc"]] = todo.get(tk["acc"], 0) + 1
+
+    def wait(q, toks):
+        need = {}
+        for s, v in toks:
+            need[s] = max(need.get(s, 0), v)
+        for s, v in need.items():
+            if known[q].get(s, 0) < v:
+                Q[q].wait_ge(T.sem[s], v)
+                known[q][s] = v
+
+    for k in order(tasks):
+        tk = tasks[k]
+        q = tk["q"]
+        wait(q, [tok[p][w] for p, w in tk["pre"] if w])
+        if tk["kind"] == "op":
+            s = "c" + q
+            for call in tk["body"]:
+                if tk["acc"] is not None:
+                    todo[tk["acc"]] -= 1
+                    ins = PE.matmul(call[0], call[1], call[2], False, todo[tk["acc"]] == 0)
+                else:
+                    ins = call()
+                ins.then_inc(T.sem[s], 1)
+                total[s] = total.get(s, 0) + 1
+            tok[k] = {"R": (s, total[s]), "W": (s, total[s])}
+        elif tk["kind"] == "dma":
+            s = "d%d" % nd[0]
+            nd[0] += 1
+            for out, in_ in tk["body"]:
+                Q[q].dma_start(out, in_).then_inc(T.sem[s], 16)
+            total[s] = 16 * len(tk["body"])
+            tok[k] = {"R": (s, total[s]), "W": (s, total[s])}
+        else:
+            src_of, dst_of, sa, sl = tk["body"]
+            trs = []
+            for c, eng in plans[core].items():
+                rid, pid, _e = topo.addr(c)
+                r = cores.index(c)
+                trs.append(RemoteDMATransfer(dst_ids=[DstId(rid=rid, pnc=pid)], dma_engine_mask=sum(1 << e for e in eng),
+                                             remote_sem=T.sem[sa], src=src_of(r), dst=dst_of(r)))
+            g.remote_dma_fused(trs, local_sem=T.sem[sl])
+            total[sl] = sum(len(e) for e in plans[core].values())
+            total[sa] = sum(len(plans[c][core]) for c in cores if c != core)
+            tok[k] = {"R": (sl, total[sl]), "W": (sa, total[sa])}
+    wait("g", list(total.items()))

@@ -2,58 +2,68 @@ from concourse.bass import DstId, RemoteDMATransfer
 from concourse.mybir import AluOpType as OP, AxisListType as AX, ActivationFunctionType as AF
 
 RO = 3
-WN = 32768
+WN = 34816
 MAGIC = 12582912.0
+FOUR, SPREAD = 4369, 33825
 B, F, I, U = "bfloat16", "float32", "int32", "uint16"
+G16 = "g" * 16
 CFG = {
-    "ns": 8,
-    "fill": "vvvsvvssvvssssvv" "vvvvvssvvvsggggg",
-    "gm": "sssvsvsv",
-    "gr": "svssvssv",
-    "xr": "svvvsvvsvsssvvvs",
-    "offs": ((1, 3), (0, 1), (3, 4)),
-    "sel": ((1, 3), (0, 1), (3, 4)),
-    "bump": {},
-    "early": 12000.0, "ahead": 3, "xw": "vvsssvss", "xr0": "vvvvvvsvsvssvsvv",
-    "gm3": "ssvvssvs", "gr3": "vssvssss", "offs3": ((1, 3), (0, 1), (3, 4)),
-    "g": 1.5, "pe": 0.5, "dma": 1900.0, "rem": 2600.0, "link": 150.0, "delta": 120.0,
+    "vote": ("ssssssaaaavvvvvv", "ssssaaaaaaaaaavv", "ssssaaaaaaaaaavv"),
+    "fill": "vvvssddvdsgvddvdgdsgdddvdsdvvggsgg",
+    "offs": (((0, 1), (1, 5), (5, 7), (7, 8)),) * 2 + (((0, 2), (2, 4), (4, 7), (7, 8)),),
+    "sel": (((0, 1), (1, 5), (5, 8)),) * 2 + (((0, 2), (2, 4), (4, 6), (6, 8)),),
+    "prep": ((0, 6), (6, 8)), "store": ((0, 6), (6, 8)),
+    "in": ((0, 5), (5, 8)), "out": ((0, 2), (2, 4), (4, 6), (6, 8)),
+    "xr": ((192, 384, "svssvsvvssvsvvvv"), (384, 512, G16)),
+    "xr2": ((128, 320, G16), (320, 512, G16)),
+    "both": ("DM1 DM5 G0 G1 G2 G4 G5 G6 G7",) * 2 + ("DM2 DM3 DM6 G1 G2 G4 G6",),
+    "cut": (9, 16, 16),
+    "xw": "vvsvvssv",
+    "lead": (-10.1, -9.4, -1.2, -0.8, 14.0, 4.0), "lead3": (-3.0, -2.1, 4.0, 5.4), "swap": 1004.0, "side": 15.0,
+    "hold": 1, "wait": 1, "early": 6000.0, "ahead": 3, "passes": 2, "delta": 0.2,
 }
+ORDER = []
+COST = {"cyc": 0.83, "g": 1.56, "pe": 0.42, "dma": 900.0, "kb": 1.5, "row": 0.7, "rem": 1600.0, "link": 200.0, "call": 400.0,
+        "op": -35.0, "sem": 140.0, "iss": 40.0}
 
 SCRATCH = {
     "RW": ("sbuf", [128, WN], B), "XW": ("sbuf", [128, 4096], B), "MW": ("sbuf", [128, 4096], B),
-    "D": ("sbuf", [128, 8192], B), "G": ("sbuf", [128, 8192], B),
+    "D": ("sbuf", [128, 8192], B), "G": ("sbuf", [128, 8192], B), "DM": ("sbuf", [128, 8192], B),
     "XR": ("sbuf", [128, 8192], B), "RL": ("sbuf", [128, 8192], B),
-    "X": ("sbuf", [128, 512], B), "X2": ("sbuf", [128, 512], F), "XT": ("sbuf", [128, 512], B),
-    "SUM": ("sbuf", [128, 512], F), "SUM2": ("sbuf", [128, 512], F),
+    "X": ("sbuf", [128, 512], B), "XT": ("sbuf", [128, 512], B), "Y": ("sbuf", [128, 512], B),
     "ROT": ("sbuf", [128, 512], I), "R16": ("sbuf", [128, 512], U), "R16b": ("sbuf", [128, 512], U),
-    "RF": ("sbuf", [128, 512], F), "RI": ("sbuf", [128, 512], I), "FAR": ("sbuf", [128, 512], U),
+    "RF": ("sbuf", [128, 512], F), "FAR": ("sbuf", [128, 512], U),
     "OFF": ("sbuf", [128, 512], U), "HI": ("sbuf", [128, 512], B), "LO": ("sbuf", [128, 512], B),
-    "SG": ("sbuf", [128, 512], F), "SJ": ("sbuf", [128, 512], I), "BS": ("sbuf", [128, 512], I),
+    "SG": ("sbuf", [128, 512], B),
     "TA": ("sbuf", [128, 512], I), "TC": ("sbuf", [128, 512], I), "TF": ("sbuf", [128, 512], F),
-    "TD": ("sbuf", [128, 512], I), "TE": ("sbuf", [128, 512], I),
-    "SO": ("sbuf", [128, 512], F), "MB": ("sbuf", [128, 512], B),
+    "SO": ("sbuf", [128, 512], F), "KR": ("sbuf", [128, 128], B),
     "KI": ("sbuf", [128, 32], I), "KP": ("sbuf", [128, 32], I), "KK": ("sbuf", [128, 32], I),
     "PB": ("sbuf", [128, 32], B), "KB": ("sbuf", [128, 32], B), "KT": ("sbuf", [128, 256], B),
-    "DL": ("sbuf", [128, 32], U), "ML": ("sbuf", [128, 32], U), "MI": ("sbuf", [128, 32], I), "MJ": ("sbuf", [128, 32], I),
+    "DL": ("sbuf", [128, 32], U), "MI": ("sbuf", [128, 8], I), "MJ": ("sbuf", [128, 8], I),
     "CNT": ("sbuf", [128, 16], F), "LAND": ("sbuf", [128, 24], F), "TOT": ("sbuf", [128, 4], F),
     "IWv": ("sbuf", [128, 240], F), "IW": ("sbuf", [128, 240], B), "BOv": ("sbuf", [128, 128], F),
     "BOc": ("sbuf", [128, 128], F), "BO": ("sbuf", [128, 128], B), "TB": ("sbuf", [128, 512], B),
     "RM": ("sbuf", [128, 512], B), "C256": ("sbuf", [128, 32], B), "PI": ("sbuf", [128, 4], I), "PJ": ("sbuf", [128, 4], I),
-    "PW": ("sbuf", [128, 8], F), "SPi": ("sbuf", [128, 16], I), "SPj": ("sbuf", [128, 16], I), "SP": ("sbuf", [128, 16], B),
-    "GI": ("sbuf", [128, 8], F), "SEL": ("sbuf", [128, 1024], B), "EE": ("sbuf", [128, 2048], B), "WT": ("sbuf", [128, 6 * 144], B),
+    "PW": ("sbuf", [128, 12], F), "KS": ("sbuf", [128, 512], B), "KSv": ("sbuf", [128, 512], B),
+    "BR": ("sbuf", [128, 128], B), "ONE": ("sbuf", [128, 8], F), "IH": ("sbuf", [128, 128], B), "CN": ("sbuf", [128, 512], B),
+    "GI": ("sbuf", [128, 8], F), "SEL": ("sbuf", [128, 1024], B), "EE": ("sbuf", [128, 2048], B), "WT": ("sbuf", [128, 3 * 144], B),
+    "WK": ("sbuf", [128, 8], B), "WR": ("sbuf", [128, 32], B), "IL": ("sbuf", [128, 240], B), "ER": ("sbuf", [128, 8 * 240], B),
     "SX": ("dram", [8, 128, 64], B), "LX": ("dram", [8, 128, 64], B),
-    "SR": ("dram", [8, 128, 64], U), "LR": ("dram", [8, 128, 64], U),
     "SX2": ("dram", [8, 128, 64], B), "LX2": ("dram", [8, 128, 64], B),
-    "SO4": ("dram", [32, 128, 16], F), "LO4": ("dram", [32, 128, 16], F),
-    "DX": ("dram", [16, 8, 512], B), "DR": ("dram", [4, 16, 2048], B),
+    "DX": ("dram", [16, 8, 512], B), "DR": ("dram", [4, 17, 2048], B),
 }
+for _q, (_a, _b) in enumerate(CFG["in"]):
+    SCRATCH["SR%d" % _q] = SCRATCH["LR%d" % _q] = ("dram", [8, 128, 8 * (_b - _a)], U)
+for _q, (_a, _b) in enumerate(CFG["out"]):
+    SCRATCH["SO%d" % _q] = SCRATCH["LO%d" % _q] = ("dram", [8, 128, 8 * (_b - _a)], F)
 for _b in range(8):
     SCRATCH["ps%d" % _b] = ("psum", [128, 512], F)
 
-SEMAPHORES = (["cv", "cs", "cp", "cg", "ax", "lx", "ar", "lr", "ax2", "lx2"]
-              + ["ae%d" % t for t in range(RO)] + ["le%d" % t for t in range(RO)]
-              + ["ao%d" % q for q in range(4)] + ["lo%d" % q for q in range(4)]
-              + ["d%d" % k for k in range(60)])
+SEMAPHORES = (["cv", "cs", "cp", "cg", "ax", "lx", "ax2", "lx2"]
+              + [k + "r%d" % q for q in range(len(CFG["in"])) for k in "al"]
+              + [k + "e%d" % t for t in range(RO) for k in "al"]
+              + [k + "o%d" % q for q in range(len(CFG["out"])) for k in "al"]
+              + ["d%d" % k for k in range(70)])
 
 
 def engine_plan(topo, cores, src):
@@ -71,39 +81,104 @@ def engine_plan(topo, cores, src):
     return plan
 
 
-def order(tasks):
+def times(tk, C):
+    kind, a, b, c = tk["cost"]
+    if kind == "op":
+        return (max(a + b * C["g"], 64) * C["cyc"] + c + C["op"], 0.0, C["sem"])
+    if kind == "pe":
+        return (a * C["pe"], 0.0, 60.0 + C["sem"])
+    if kind == "dma":
+        return (C["iss"] * a, b * C["kb"] + c * C["row"], C["dma"])
+    return (C["call"], C["link"] * a, C["rem"])
+
+
+def place(tm, before, rank):
+    n = len(tm)
+    after = [[] for _ in range(n)]
+    left = [len(before[k]) for k in range(n)]
+    for k in range(n):
+        for p, _gap in before[k]:
+            after[p].append(k)
+    ready = [k for k in range(n) if left[k] == 0]
+    start, busy = [0.0] * n, {}
+    while ready:
+        k = min(ready, key=lambda j: rank[j])
+        ready.remove(k)
+        s, moved = max([start[p] + gap for p, gap in before[k]], default=0.0), True
+        while moved:
+            moved = False
+            for q, off, d in tm[k]:
+                for a, b in busy.get(q, ()):
+                    if a < s + off + d and s + off < b:
+                        s, moved = b - off, True
+        start[k] = s
+        for q, off, d in tm[k]:
+            busy.setdefault(q, []).append((s + off, s + off + d))
+        for j in after[k]:
+            left[j] -= 1
+            if left[j] == 0:
+                ready.append(j)
+    return start
+
+
+def forward(tasks, tm, rank):
     n = len(tasks)
-    succ = [[] for _ in range(n)]
+    succ = [set() for _ in range(n)]
     for k, t in enumerate(tasks):
         for p, _w in t["pre"]:
-            succ[p].append(k)
-    level = [0.0] * n
-    for k in range(n - 1, -1, -1):
-        level[k] = tasks[k]["hold"] + tasks[k]["lat"] + tasks[k].get("early", 0.0) + max([level[s] for s in succ[k]], default=0.0)
-    for k, d in CFG["bump"].items():
-        level[k] += d
+            succ[p].add(k)
     left = [len(set(p for p, _w in t["pre"])) for t in tasks]
-    succ = [sorted(set(s)) for s in succ]
-    est, free, out = {}, {}, []
+    est, free, out = {k: 0.0 for k in range(n) if left[k] == 0}, {}, []
     fin, end = [0.0] * n, [0.0] * n
-    for k in range(n):
-        if left[k] == 0:
-            est[k] = 0.0
     while est:
-        t0, q = min((max(e, free.get(tasks[k]["q"], 0.0)), tasks[k]["q"]) for k, e in est.items())
-        k = max((level[k], -k) for k, e in est.items() if tasks[k]["q"] == q and e <= t0 + CFG["delta"])
-        k = -k[1]
-        st = max(est.pop(k), free.get(q, 0.0))
-        end[k] = free[q] = st + tasks[k]["hold"]
-        fin[k] = end[k] + tasks[k]["lat"]
-        out.append(k)
-        tasks[k]["at"] = st
+        t0, q = min((max(e, free.get(x, 0.0)), x) for k, e in est.items() for x in tasks[k]["q"])
+        mine = sorted((rank[k], k) for k in est if q in tasks[k]["q"])
+        now = [k for _r, k in mine if est[k] <= t0][0]
+        k = [j for _r, j in mine if est[j] <= t0 + CFG["delta"] * tm[now][0]][0]
+        end[k] = free[q] = max(est.pop(k), free.get(q, 0.0)) + tm[k][0]
+        fin[k] = end[k] + tm[k][2]
+        if tm[k][1]:
+            free["engines"] = max(free.get("engines", 0.0), end[k]) + tm[k][1]
+            fin[k] = free["engines"] + tm[k][2]
+        out.append((k, q))
         for s in succ[k]:
             left[s] -= 1
             if left[s] == 0:
                 est[s] = max(fin[p] if w else end[p] for p, w in tasks[s]["pre"])
-    CFG["span"] = max(fin)
-    return out
+    return out, fin
+
+
+def order(tasks, C):
+    if ORDER:
+        return ORDER
+    n = len(tasks)
+    tm = [times(t, C) for t in tasks]
+    whole = [sum(x) + t.get("early", 0.0) for t, x in zip(tasks, tm)]
+    pre, post = [{} for _ in range(n)], [{} for _ in range(n)]
+    for k, t in enumerate(tasks):
+        for p, w in t["pre"]:
+            pre[k][p] = max(pre[k].get(p, 0.0), whole[p] if w else tm[p][0])
+    for k in range(n):
+        for p, gap in pre[k].items():
+            post[p][k] = whole[k] - whole[p] + gap
+    post = [list(d.items()) for d in post]
+    back, best = place([()] * n, post, range(n)), None
+    for _ in range(CFG["passes"]):
+        rank = [-(back[k] + whole[k]) for k in range(n)]
+        for k, t in enumerate(tasks):
+            if "wave" in t:
+                rank[k] = 1000.0 * t["wave"][0] + t["wave"][1] + 1e-4 * k
+        out, fin = forward(tasks, tm, rank)
+        if best is None or max(fin) < best[0]:
+            best = (max(fin), out)
+        bw = [None] * n
+        for k, q in out:
+            bw[k] = [(q, whole[k] - tm[k][0], tm[k][0])]
+            if tm[k][1]:
+                bw[k].append(("engines", whole[k] - tm[k][0] - tm[k][1], tm[k][1]))
+        back = place(bw, post, [-x for x in fin])
+    ORDER.extend(best[1])
+    return ORDER
 
 
 def rank_program(g, core, T, topo):
@@ -111,13 +186,11 @@ def rank_program(g, core, T, topo):
     if me is None:
         return
     cores = list(T.cores)
-    NS, GC = CFG["ns"], CFG["g"]
     Q = {"v": g.vector, "s": g.scalar, "p": g.tensor, "y": g.sync, "g": g}
-    tasks, writer, readers, bank, base = [], {}, {}, {}, {}
+    tasks, writer, readers, bank, base, wave = [], {}, {}, {}, {}, []
 
-    def task(q, kind, body, hold, lat, R=(), W=(), P=(), acc=None):
+    def task(q, kind, body, cost, R=(), W=(), P=(), acc=None):
         k = len(tasks)
-        same = lambda p: kind == "op" and tasks[p]["kind"] == "op" and tasks[p]["q"] == q
         pre = [(writer[x], "W") for x in R if x in writer]
         for x in W:
             if x in writer:
@@ -127,301 +200,368 @@ def rank_program(g, core, T, topo):
             if acc is not None and acc not in base:
                 base[acc] = list(bank.get(b, []))
                 bank[b] = []
-            pre += [(p, None if same(p) else "W") for p in (base[acc] if acc is not None else bank.get(b, []))]
+            pre += [(p, None if tasks[p]["q"] == q == "p" else "W") for p in (base[acc] if acc is not None else bank.get(b, []))]
             bank[b] = (bank[b] if acc is not None else []) + [k]
-        tasks.append({"q": q, "kind": kind, "body": body, "hold": hold, "lat": lat, "pre": pre, "acc": acc,
+        tasks.append({"q": q, "kind": kind, "body": body, "cost": cost, "pre": pre, "acc": acc,
                       "name": (list(W) + list(P) + ["-"])[0]})
+        if wave:
+            tasks[-1]["wave"] = tuple(wave)
         for x in R:
             readers.setdefault(x, []).append(k)
         for x in W:
             writer[x] = k
             readers[x] = []
 
-    def op(q, call, d, R=(), W=(), P=()):
-        task(q, "op", [call], max(d, 64) + (60 if d > 64 else 20), 100, R, W, P)
+    def op(q, call, d, R=(), W=(), P=(), gat=0):
+        task(q, "op", [call], ("op", d, gat, 150 if q == "g" else 60 if d + gat > 64 else 20), R, W, P)
 
-    def dma(q, moves, kb, R=(), W=(), early=0.0):
-        task(q, "dma", moves, 60 * len(moves), CFG["dma"] + 4 * kb, R, W)
+    def dma(q, moves, kb, rows, R=(), W=(), early=0.0):
+        task(q, "dma", moves, ("dma", len(moves), kb, rows), R, W)
         tasks[-1]["early"] = early
 
     def exchange(src_of, dst_of, sa, sl, kb, R, W):
-        task("g", "rem", (src_of, dst_of, sa, sl), 600 + CFG["link"] * kb, CFG["rem"], R, W)
+        task("g", "rem", (src_of, dst_of, sa, sl), ("rem", kb, 0, 0), R, W)
 
     V, S, PE = g.vector, g.scalar, g.tensor
     ps = [T["ps%d" % b] for b in range(8)]
     ID = T.IW[:, 112:240]
     blk = lambda n, a, b: [(n, c) for c in range(a, b)]
-    rng4 = lambda n: blk(n, 0, 4)
+    all8 = lambda n: blk(n, 0, 8)
 
     def ts(d, out, in0, a, b, o0, o1=None, R=(), W=(), P=()):
         if o1 is None:
-            op("v", lambda: V.tensor_scalar(out, in0, a, None, o0), d, R, W, P)
+            op("v", lambda q: V.tensor_scalar(out, in0, a, None, o0), d, R, W, P)
         else:
-            op("v", lambda: V.tensor_scalar(out, in0, a, b, o0, o1), d, R, W, P)
+            op("v", lambda q: V.tensor_scalar(out, in0, a, b, o0, o1), d, R, W, P)
 
-    def tt(d, out, in0, in1, o, R=(), W=(), P=()):
-        op("v", lambda: V.tensor_tensor(out, in0, in1, o), d, R, W, P)
+    def tt(d, out, in0, in1, o, R=(), W=(), P=(), gat=0):
+        op("v", lambda q: V.tensor_tensor(out, in0, in1, o), d, R, W, P, gat)
 
-    def cp(d, out, in_, R=(), W=(), P=()):
-        op("v", lambda: V.tensor_copy(out, in_), d, R, W, P)
-
-    def act(d, out, in_, fn, R=(), W=(), P=(), **kw):
-        op("s", lambda: S.activation(out, in_, fn, **kw), d, R, W, P)
+    def cp(who, d, out, in_, R=(), W=(), P=(), gat=0):
+        op(who, lambda q: V.tensor_copy(out, in_) if q == "v" else S.activation(out, in_, AF.Copy), d, R, W, P, gat)
 
     def mms(b, n, lst, R, acc=None):
-        task("p", "op" if acc is None else "op", [(lambda a=a: PE.matmul(*a)) for a in lst] if acc is None else lst,
-             max(n, 64) * CFG["pe"] * len(lst), 160, R, (), (b,), acc)
+        task("p", "op", [(lambda q, a=a: PE.matmul(*a)) for a in lst] if acc is None else lst,
+             ("pe", max(n, 64) * len(lst), 0, 0), R, (), (b,), acc)
 
-    def iota(d, out, pattern, base_, cm, W):
-        op("g", lambda: g.iota(out, pattern, base_, cm, allow_small_or_imprecise_dtypes=True), 2 * d + 80, (), W)
+    def iota(d, out, pattern, base_, cm, W, R=()):
+        op("g", lambda q: g.iota(out, pattern, base_, cm, allow_small_or_imprecise_dtypes=True), 2 * d, R, W)
 
     wt = lambda k, c: T.WT[:, 144 * k + 15 - c:144 * k + 143 - c]
-    W_RELU, W_NEG, W_ABS, W_M, W_SUM, W_DIF = range(6)
+    W_RELU, W_NEG, W_ABS = range(3)
 
-    dma("y", [(T.SX[:], T.x[:])], 128, (), ["SX"])
-    dma("s", [(T.ROT[:], T.rot[:])], 256, (), ["ROT"])
-    dma("y", [(T.LX[me], T.x[16 * me:16 * me + 16, :])], 16, (), ["LXo"])
+    dma("y", [(T.SX[:], T.x[:])], 128, 16, (), ["SX"])
+    for h, (ha, hb) in enumerate(CFG["in"]):
+        dma("s", [(T.ROT[:, 64 * ha:64 * hb], T.rot[:, 64 * ha:64 * hb])], 32 * (hb - ha), 128, (), [("ROT", h)])
+    dma("y", [(T.LX[me], T.x[16 * me:16 * me + 16, :])], 16, 16, (), ["LXo"])
     iota(240, T.IWv[:], [[1, 240]], -112, -1, ["IWv"])
     iota(128, T.BOv[:], [[-16, 8], [0, 16]], 0, 1, ["BOv"])
-    op("g", lambda: g.iota(T.PI[:, 0:1], [[0, 1]], 0, 1), 100, (), ["PI"])
-    iota(32, T.C256[:], [[256, 32]], 0, 0, ["C256"])
+    op("g", lambda q: g.iota(T.PI[:, 0:1], [[0, 1]], 0, 1), 1, (), ["PI"])
+    iota(32, T.C256[:], [[-256, 32]], 0, 0, ["C256"])
+    iota(512, T.KSv[:], [[1, 4], [0, 4], [4, 32]], 0, -1, ["KSv"])
     iota(512, T.TB[:], [[0, 32], [-1, 16]], 15, 0, ["TB"])
-    exchange(lambda r: T.SX[r], lambda r: T.LX[me], "ax", "lx", 16, ["SX"], ["LX"])
-    cp(512, T.R16[:], T.ROT[:], ["ROT"], ["R16"])
-    dma("y", [(T.SR[:], T.R16[:])], 128, ["R16"], ["SR"])
-    dma("y", [(T.LR[me], T.R16[16 * me:16 * me + 16, :])], 16, ["R16"], ["LRo"])
-    exchange(lambda r: T.SR[r], lambda r: T.LR[me], "ar", "lr", 16, ["SR"], ["LR", "sent"])
+    for h, (ha, hb) in enumerate(CFG["in"]):
+        cp("v", 64 * (hb - ha), T.R16[:, 64 * ha:64 * hb], T.ROT[:, 64 * ha:64 * hb], [("ROT", h)], [("R16", h)])
+    exchange(lambda r: T.SX[r], lambda r: T.LX[me], "ax", "lx", 16, ["SX"] + blk("R16", 0, CFG["hold"]), ["LX"])
+    sent = len(tasks) - 1
+    dma("y", [(T.X[:], T.LX[:])], 128, 128, ["LX", "LXo"], ["X"])
+    for h, (ha, hb) in enumerate(CFG["in"]):
+        a, b, w, sr, lr = 64 * ha, 64 * hb, hb - ha, T["SR%d" % h], T["LR%d" % h]
+        dma("y", [(sr[:], T.R16[:, a:b]), (lr[me], T.R16[16 * me:16 * me + 16, a:b])], 18 * w, 144, [("R16", h)], [("SR", h)])
+        exchange(lambda r, sr=sr: sr[r], lambda r, lr=lr: lr[me], "ar%d" % h, "lr%d" % h, 2 * w,
+                 [("SR", h)] + ["LX"] * (h > 0 and CFG["wait"]), [("LR", h)])
+        tasks[-1]["pre"].append((sent, None))
+        dma("y", [(T.R16b[:, a:b], lr[:])], 16 * w, 128, [("LR", h), ("SR", h)], [("R16b", h)])
+    LAST = ("R16b", len(CFG["in"]) - 1)
     k = 0
-    while k < 32:
+    while k < 34:
         q, n = CFG["fill"][k], 1
-        while q != "s" and k + n < 32 and CFG["fill"][k + n] == q and (q == "g" or n < 2):
+        while q != "s" and k + n < 34 and CFG["fill"][k + n] == q and n < 2:
             n += 1
         w = T.RW[:, 1024 * k:1024 * (k + n)]
-        if q == "v":
-            op("v", lambda w=w: V.memset(w, 0.0), 512 * n, (), blk("Z", k, k + n))
+        if q == "d":
+            dma("y", [(w, T.RW[:, 0:1024 * n])], 256 * n, 128, blk("Z", 0, n) + [LAST], blk("Z", k, k + n))
+        elif q == "v":
+            op("v", lambda q, w=w: V.memset(w, 1.0), 512 * n, (), blk("Z", k, k + n))
         elif q == "s":
-            act(1024, w, T.RW[:, 0:1024], AF.Copy, [("Z", 0)], [("Z", k)])
+            cp("s", 1024, w, T.RW[:, 0:1024], [("Z", 0)], [("Z", k)])
         else:
-            op("g", lambda w=w, n=n: g.iota(w, [[0, 1024 * n]], 0, 0, allow_small_or_imprecise_dtypes=True),
-               2048 * n, ["SR"], blk("Z", k, k + n))
+            iota(1024 * n, w, [[0, 1024 * n]], 1, 0, blk("Z", k, k + n), [("SR", 0)])
         k += n
-    op("g", lambda: g.iota(T.MW[:], [[0, 4096]], 0, 0, allow_small_or_imprecise_dtypes=True), 8192, ["SR"], ["MWv", "MWs"])
+    op("v", lambda q: V.memset(T.MW[:], 0.0), 2048, (), ["MW"])
+    dma("y", [(T.MW[1 + r:128:16, 512 * r:512 * r + 512], T.RW[0:8, 0:512]) for r in range(8)], 64, 64, [("Z", 0), LAST], ["MW"])
+    dma("y", [(T.DR[0:2, 16, :], T.RW[0:4, 0:1024]), (T.DR[2:4, 0, :], T.RW[0:4, 0:1024])], 16, 8, [("Z", 0)], ["DR0"])
 
     ts(240, T.IW[:], T.IWv[:], 0.0, None, OP.is_equal, None, ["IWv"], ["IW"])
     ts(128, T.BOc[:], T.BOv[:], 0.0, 15.0, OP.max, OP.min, ["BOv"], ["BOc"])
-    op("v", lambda: V.memset(T.WT[:], 0.0), 432, (), ["WT0"])
+    op("v", lambda q: V.memset(T.WT[:], 0.0), 216, (), ["WT0"])
+    op("v", lambda q: V.memset(T.CN[:], -15.0 / 64), 256, (), ["CN"])
     ts(1, T.PJ[:, 0:1], T.PI[:, 0:1], 15, None, OP.bitwise_and, None, ["PI"], ["PJ"])
     ts(256, T.RM[:], T.TB[:], 15.0, None, OP.not_equal, None, ["TB"], ["RM"])
     tt(256, T.BO[:], T.BOc[:], T.BOv[:], OP.is_equal, ["BOc", "BOv"], ["BO"])
-    ts(16, T.SPi[:], T.TB[:, 0:16], -17.0, 255.0, OP.mult, OP.add, ["TB"], ["SPi"])
-    ts(1, T.PW[:, 0:1], T.PJ[:, 0:1], 16.0, None, OP.mult, None, ["PJ"], ["PW0"])
-    ts(1, T.PW[:, 1:2], T.PJ[:, 0:1], 0.0, None, OP.is_equal, None, ["PJ"], ["PW1"])
-    ts(1, T.PW[:, 2:3], T.PJ[:, 0:1], 4.0, 0.5, OP.is_lt, OP.mult, ["PJ"], ["PW2"])
-    ts(1, T.PW[:, 3:4], T.PJ[:, 0:1], 2.0, None, OP.is_lt, None, ["PJ"], ["PW3"])
-    op("v", lambda: V.memset(T.SPi[:, 0:1], 255), 1, ["SPi"], ["SPi"])
-    tt(1, T.PW[:, 4:5], T.PW[:, 2:3], T.PW[:, 3:4], OP.subtract, ["PW2", "PW3"], ["PW4"])
-    for k, w in enumerate((32.0, -16.0, 16.0, T.PW[:, 1:2], T.PW[:, 2:3], T.PW[:, 4:5])):
-        ts(8, T.WT[:, 144 * k + 15:144 * k + 143:16], T.BO[:, 0:128:16], w, None, OP.mult, None,
-           ["BO", "WT0", "PW1", "PW2", "PW4"], [("WT", k)])
-    ts(16, T.SPj[:], T.SPi[:], 165, None, OP.bitwise_and, None, ["SPi"], ["SPj"])
+    ts(64, T.IH[:], ID, 0.5, None, OP.mult, None, ["IW"], ["IH"])
+    place_ = T.PJ[:, 0:1]
+    pw = lambda k: T.PW[:, k:k + 1]
+    ts(1, pw(0), place_, 16.0, 15.0, OP.mult, OP.add, ["PJ"], [("PW", 0)])
+    ts(1, pw(2), place_, 2.0, None, OP.is_lt, None, ["PJ"], [("PW", 2)])
+    ts(1, pw(3), place_, 4.0, -0.5, OP.is_lt, OP.mult, ["PJ"], [("PW", 3)])
+    ts(1, pw(4), pw(3), pw(2), 2.0 ** -13, OP.add, OP.mult, [("PW", 2), ("PW", 3)], [("PW", 4)])
+    ts(1, pw(5), place_, -1.0, 15.0, OP.mult, OP.add, ["PJ"], [("PW", 5)])
+    ts(1, pw(6), T.PI[:, 0:1], pw(5), -15.0, OP.add, OP.add, ["PI", ("PW", 5)], [("PW", 6)])
+    ts(1, pw(7), place_, 4.0, -32768.0, OP.is_equal, OP.mult, ["PJ"], [("PW", 7)])
+    ts(1, pw(8), pw(7), pw(2), 2.0, OP.add, OP.mult, [("PW", 2), ("PW", 7)], [("PW", 8)])
+    ts(1, pw(9), pw(4), 2.0, None, OP.mult, None, [("PW", 4)], [("PW", 9)])
+    ts(1, pw(1), pw(6), -0.0625, 14.0, OP.mult, OP.add, [("PW", 6)], [("PW", 1)])
+    GC8 = T.BO[:, 0:128:16]
+    for k, w in enumerate((32.0, -16.0, 16.0)):
+        ts(8, T.WT[:, 144 * k + 15:144 * k + 143:16], GC8, w, None, OP.mult, None, ["BO", "WT0"], [("WT", k)])
+    ts(64, T.BR[:], T.TB[:, 0:128], pw(1), None, OP.is_equal, None, ["TB", ("PW", 1)], ["BR"])
+    ts(256, T.KS[:], T.KSv[:], 0.0, None, OP.is_equal, None, ["KSv"], ["KS"])
+    op("v", lambda q: V.memset(T.ONE[:], 1.0), 8, (), ["ONE"])
+    for k, w in enumerate((2, 4, 8, 9)):
+        a = 16 * (k // 2) + k % 2
+        ts(8, T.WR[:, a:a + 15:2], GC8, pw(w), None, OP.mult, None, ["BO", ("PW", w)], [("WR", k)])
     for i in range(16):
         ts(64, T.EE[:, i:2048:16], ID, -1.0, None, OP.mult, None, ["IW"], [("EE", i)])
-    cp(16, T.SP[:], T.SPj[:], ["SPj"], ["SP"])
 
-    dma("y", [(T.X[:], T.LX[:])], 128, ["LX", "LXo"], ["X"])
-    dma("y", [(T.R16b[:], T.LR[:])], 128, ["LR", "LRo"], ["R16b"])
     XWK = blk("XW", 0, 8)
-    ts(1, T.PW[:, 5:6], T.PJ[:, 0:1], -1.0, 15.0, OP.mult, OP.add, ["PJ"], ["PW5"])
-    cp(8, T.GI[:], T.BO[:, 0:128:16], ["BO"], ["GI"])
+    cp("v", 8, T.GI[:], GC8, ["BO"], ["GI"])
     for r in range(8):
         sel = T.SEL[:, 128 * r:128 * r + 128]
-        ts(64, sel, T.TB[:, 0:128], T.PW[:, 5:6], T.GI[:, r:r + 1], OP.is_equal, OP.mult,
-           ["TB", "PW5", "GI"], [("SEL", r)])
-        b, out = (0, 1, 2, 3, 4, 5, 7, 0)[r], T.XW[:, 512 * r:512 * r + 512]
+        ts(64, sel, T.TB[:, 0:128], pw(5), T.GI[:, r:r + 1], OP.is_equal, OP.mult, ["TB", ("PW", 5), "GI"], [("SEL", r)])
+        b = (0, 1, 2, 3, 4, 6, 1, 0)[r]
         mms(b, 512, [(ps[b][:], sel, T.X[:], True, True)], [("SEL", r), "X"])
-        if CFG["xw"][r] == "v":
-            cp(512, out, ps[b][:], (), [("XW", r)], (b,))
-        else:
-            act(512, out, ps[b][:], AF.Copy, (), [("XW", r)], (b,))
+        cp(CFG["xw"][r], 512, T.XW[:, 512 * r:512 * r + 512], ps[b][:], (), [("XW", r)], (b,))
+    ts(240, T.IL[:], T.IWv[:], pw(6), 0.0, OP.add, OP.is_equal, ["IWv", ("PW", 6)], ["IL"])
+    for r in range(8):
+        ts(120, T.ER[:, 240 * r:240 * r + 240], T.IL[:], T.GI[:, r:r + 1], None, OP.mult, None, ["IL", "GI"], [("ER", r)])
 
-    def x_window_load(after):
-        dma("y", [(T.XW[16 * r:16 * r + 16, :], T.DX[:]) for r in range(8)], 1024, ["DX"] + after, XWK)
+    def runs(s):
+        cut = [k for k in range(len(s)) if k == 0 or s[k] != s[k - 1]] + [len(s)]
+        return [(a, b, s[a]) for a, b in zip(cut, cut[1:])]
 
-    v0 = 32 * NS
+    def x_forms(t, jobs):
+        vbs = sorted(set(c // 4 for c in range(16) if CFG["vote"][t][c] == "s"))
+        mms(7, 128, [(ps[7][:, 128 * vb:128 * vb + 128], T.X[:, 128 * vb:128 * vb + 128], ID, True, True)
+                     for vb in vbs], ["X", "IW"])
+        a, b = 128 * vbs[0], 128 * vbs[-1] + 128
+        cp("s", b - a, T.XT[:, a:b], ps[7][:, a:b], (), ["XT"], (7,))
+        for a, b, who in jobs:
+            for i in range(16):
+                out, in_, W = T.XR[:, 16 * a + i:16 * b:16], T.X[:, a:b], [("XR", c, i) for c in range(a // 32, b // 32)]
+                if who[i] == "g":
+                    op("g", lambda q, out=out, in_=in_, n=b - a: g.affine_select(out, in_, [[0, n]], OP.is_ge, 0.0, 0, 0),
+                       2 * (b - a), ["X"], W)
+                else:
+                    cp(who[i], (b - a) // (2 if who[i] == "v" else 1), out, in_, ["X"], W)
 
-    def x_forms(who):
-        act(512 - v0, T.X2[:, v0:512], T.X[:, v0:512], AF.Identity, ["X"], ["X2b"], scale=2.0)
-        nb = (NS + 3) // 4
-        mms(6, 128, [(ps[6][:, 128 * vb:128 * vb + 128], T.X[:, 128 * vb:128 * vb + 128], ID, True, True)
-                     for vb in range(nb)], ["X", "IW"])
-        act(128 * nb, T.XT[:, 0:128 * nb], ps[6][:, 0:128 * nb], AF.Copy, (), ["XT"], (6,))
-        for i in range(16):
-            out, in_ = T.XR[:, 16 * v0 + i:8192:16], T.X[:, v0:512]
-            if who[i] == "v":
-                cp((512 - v0) // 2, out, in_, ["X"], [("XR", i)])
-            else:
-                act(512 - v0, out, in_, AF.Copy, ["X"], [("XR", i)])
+    def lists_and_digits(ha, hb, src, P):
+        a, b = 64 * ha, 64 * hb
+        ts(b - a, T.FAR[:, a:b], src, 0.125, -4096.46875, OP.mult, OP.add, (), blk("FAR", ha, hb), P)
+        wave[1] += CFG["lead"][5]
+        cp("s", b - a, T.HI[:, a:b], src, (), blk("HI", ha, hb), P)
+        tt(b - a, T.LO[:, a:b], src, T.HI[:, a:b], OP.subtract, blk("HI", ha, hb), blk("LO", ha, hb), P)
 
-    def lists_and_digits(qa, qb, src, sk):
-        a, b = 128 * qa, 128 * qb
-        ts(b - a, T.FAR[:, a:b], src[:, a:b], 0.0625, -0.46875, OP.mult, OP.add, sk, blk("FAR", qa, qb))
-        act(b - a, T.HI[:, a:b], T.RF[:, a:b], AF.Copy, blk("RF", qa, qb), blk("HI", qa, qb))
-        tt(2 * (b - a), T.LO[:, a:b], T.RF[:, a:b], T.HI[:, a:b], OP.subtract, blk("RF", qa, qb) + blk("HI", qa, qb),
-           blk("LO", qa, qb))
+    def r_load(a, b):
+        dma("y", [(T.RW[16 * r:16 * r + 4, 2048 * a:2048 * b], T.DR[:, a:b, :]) for r in range(8)], 128 * (b - a), 128,
+            all8("DR") + ["DR0"], blk("Z", 2 * a, 2 * b), CFG["early"])
 
-    def r_window_load(h, after):
-        a, b = h * WN // 2, (h + 1) * WN // 2
-        dma("y", [(T.RW[16 * r:16 * r + 4, a:b], T.DR[:, 8 * h:8 * h + 8, :]) for r in range(8)], 1024, ["DR"] + after,
-            blk("Z", 16 * h, 16 * h + 16), CFG["early"] if h == 0 else 0.0)
+    def r_forms(parts, t):
+        for ha, hb in parts:
+            a, b = 64 * ha, 64 * hb
+            dma("y", [(T.DR[2 * (r // 4) + d, r // 4:16 + r // 4, 512 * (r % 4) + a:512 * (r % 4) + b],
+                       buf[16 * r:16 * r + 16, a:b])
+                      for d, buf in enumerate((T.HI, T.LO)) for r in range(8)], 32 * (hb - ha), 256,
+                blk("HI", ha, hb) + blk("LO", ha, hb), blk("DR", ha, hb))
+        r_load(0, CFG["cut"][t])
+        wave[:] = [t - 1, CFG["swap"]]
+        ts(256, T.SG[:], T.FAR[:], 2048.0, -16384.0, OP.is_ge, OP.mult, all8("FAR"), ["SG"])
+        er = lambda r, c: T.ER[:, 240 * r + 112 - 16 * c:240 * r + 240 - 16 * c]
+        for r in range(8):
+            for d, buf in enumerate((T.HI, T.LO)):
+                mms(6, 64, [(ps[6][:, r:512:8], T.BO[:], T.CN[:, 0:64], True, False)][d:]
+                    + [(ps[6][:, r:512:8], er(r, c), buf[:, c:512:8], False, d == 1 and c == 7) for c in range(8)],
+                    all8("HI") + all8("LO") + ["BO", "CN", ("ER", r)])
 
-    def r_window_store():
-        dma("y", [(T.DR[2 * (r // 4) + d, :, 512 * (r % 4):512 * (r % 4) + 512], buf[16 * r:16 * r + 16, :])
-                  for d, buf in enumerate((T.HI, T.LO)) for r in range(8)], 256, rng4("HI") + rng4("LO"), ["DR"])
-        r_window_load(0, [])
-
-    x_forms(CFG["xr0"])
-    cp(512, T.RF[:], T.R16b[:], ["R16b"], rng4("RF"))
-    lists_and_digits(0, 4, T.R16b, ["R16b"])
-    r_window_store()
+    x_forms(0, CFG["xr"])
+    for h, (ha, hb) in enumerate(CFG["in"]):
+        a, b, R = 64 * ha, 64 * hb, [("R16b", h)]
+        ts((b - a) // 2, T.FAR[:, a:b], T.R16b[:, a:b], 0.0625, -0.46875, OP.mult, OP.add, R, blk("FAR", ha, hb))
+        ts(b - a, ps[5][:, a:b], T.R16b[:, a:b], 0.5, 32768.0, OP.mult, OP.add, R, (), (5,))
+        cp("s", b - a, T.HI[:, a:b], ps[5][:, a:b], (), blk("HI", ha, hb), (5,))
+        tt(b - a, T.LO[:, a:b], ps[5][:, a:b], T.HI[:, a:b], OP.subtract, blk("HI", ha, hb), blk("LO", ha, hb), (5,))
+    r_forms(((0, 8),), 0)
+    wave[:] = []
 
     for t in range(RO):
+        def at(h, stage, t=t):
+            lead = CFG["lead3" if t == RO - 1 and stage < 4 else "lead"]
+            wave[:] = [] if t == 0 and stage == 4 else [t - (stage == 4), 20 + h + lead[stage]]
+
         last = t == RO - 1
-        XRK, EEK, acc = blk("XR", 0, 16), blk("EE", 0, 16), "key%d" % t
+        who = CFG["vote"][t]
+        EEK, acc = blk("EE", 0, 16), "key%d" % t
         mms(0, 512, [(ps[0][:], ID, T.TB[:], True, False)], ["IW", "TB"])
 
         def key(k, c, buf, name):
             mms(0, 512, [(ps[0][:], wt(k, c), buf[:, 512 * c:512 * c + 512])], [(name, c), ("WT", k)], acc)
 
-        first = [q for qa, qb in CFG["sel"] for q in range(qa, qb)] if t > 0 else [0, 1, 2, 3]
+        sb = (1, 2, 3, 4) if t == 0 else (1, 2)
         done = []
-        for n, c in enumerate(sorted(range(NS), key=lambda c: (first.index(c // 4), c))):
-            b = 1 + n % 4
+        for n, c in enumerate(c for c in range(16) if who[c] == "s"):
+            at(c / 2, 4)
+            b = sb[n % len(sb)]
             mms(b, 512, [(ps[b][:], T.XT[:, 128 * (c // 4):128 * (c // 4) + 128],
                           T.EE[:, 512 * (c % 4):512 * (c % 4) + 512], True, False)], ["XT"] + EEK)
-            act(512 * GC, T.D[:, 512 * c:512 * c + 512], T.XW[:, :].indirect(T.FAR[:, 32 * c:32 * c + 32]), AF.Copy,
-                XWK + [("FAR", c // 4)], [("D", c)])
+            cp("s", 0, T.D[:, 512 * c:512 * c + 512], T.XW[:, :].indirect(T.FAR[:, 32 * c:32 * c + 32]),
+               XWK + [("FAR", c // 2)], [("D", c)], gat=512)
             if n >= CFG["ahead"]:
                 tasks[-1]["pre"].append((done[n - CFG["ahead"]], None))
             mms(b, 512, [(ps[b][:], ID, T.D[:, 512 * c:512 * c + 512], False, True)], ["IW", ("D", c)])
-            act(512, T.RL[:, 512 * c:512 * c + 512], ps[b][:], AF.Abs, (), [("RL", c)], (b,))
+            op("s", lambda q, c=c, b=b: S.activation(T.RL[:, 512 * c:512 * c + 512], ps[b][:], AF.Abs), 512, (), [("RL", c)], (b,))
             done.append(len(tasks) - 1)
             key(W_ABS, c, T.RL, "RL")
-        a, done = NS, []
-        while a < 16:
-            b = a + 2 if a + 3 < 16 and a % 2 == 0 else a + 1
-            tt(512 * GC * (b - a), T.D[:, 512 * a:512 * b], T.XW[:, :].indirect(T.FAR[:, 32 * a:32 * b]),
-               T.XR[:, 512 * a:512 * b], OP.subtract, XWK + [("FAR", a // 4)] + XRK, blk("D", a, b))
+        done = []
+        vs = [c for c in range(16) if who[c] != "s"]
+        while vs:
+            a = vs[0]
+            b = a + 2 if len(vs) > 3 and a % 2 == 0 and who[a + 1] == who[a] else a + 1
+            vs = vs[b - a:]
+            at(a / 2, 4)
+            tt(0, T.D[:, 512 * a:512 * b], T.XW[:, :].indirect(T.FAR[:, 32 * a:32 * b]),
+               T.XR[:, 512 * a:512 * b], OP.subtract,
+               XWK + [("FAR", a // 2)] + [("XR", c, i) for c in range(a, b) for i in range(16)], blk("D", a, b), gat=512 * (b - a))
             if len(done) >= 2:
                 tasks[-1]["pre"].append((done[-2], None))
+            if who[a] == "a":
+                for c in range(a, b):
+                    op("s", lambda q, c=c: S.activation(T.RL[:, 512 * c:512 * c + 512], T.D[:, 512 * c:512 * c + 512], AF.Abs),
+                       512, [("D", c)], [("RL", c)])
+                    key(W_ABS, c, T.RL, "RL")
+                continue
             ts(256 * (b - a), T.RL[:, 512 * a:512 * b], T.D[:, 512 * a:512 * b], 0.0, None, OP.max, None,
                blk("D", a, b), blk("RL", a, b))
             done.append(len(tasks) - 1)
             for c in range(a, b):
                 key(W_NEG, c, T.D, "D")
                 key(W_RELU, c, T.RL, "RL")
-            a = b
-
-        op("v", lambda: V.tensor_tensor_scan(T.SO[:], T.RM[:], ps[0][:], 0.0, OP.mult, OP.max), 512, ["RM"], ["SO"], (0,))
-        cp(32, T.KI[:], T.SO[:, 15:512:16], ["SO"], ["KI"])
-        ts(32, T.KP[:], T.KI[:], 1, None, OP.bitwise_and, None, ["KI"], ["KP"])
+        wave[:] = [t, 0]
+        op("v", lambda q: V.tensor_tensor_scan(T.SO[:], T.RM[:], ps[0][:], 0.0, OP.mult, OP.max), 512, ["RM"], ["SO"], (0,))
+        cp("v", 32, T.KI[:], T.SO[:, 15:512:16], ["SO"], ["KI"])
         ts(32, T.KK[:], T.KI[:], 15, None, OP.bitwise_and, None, ["KI"], ["KK"])
-        cp(32, T.PB[:], T.KP[:], ["KP"], ["PB"])
-        ts(32, T.KB[:], T.KK[:], -1.0, 15.0, OP.mult, OP.add, ["KK"], ["KB"])
+        ts(32, T.KP[:], T.KI[:], 1, None, OP.bitwise_and, None, ["KI"], ["KP"])
+        cp("v", 32, T.KB[:], T.KK[:], ["KK"], ["KB"])
+        cp("v", 32, T.PB[:], T.KP[:], ["KP"], ["PB"])
+        mms(2, 32, [(ps[2][:, 32 * c:32 * c + 32], T.KS[:, 128 * c:128 * c + 128], T.KB[:], True, True) for c in range(4)],
+            ["KS", "KB"])
+        cp("s", 128, T.KR[:], ps[2][:, 0:128], (), ["KR"], (2,))
+        dma("y", [(T.MW[64 * h:64 * h + 64:16, :], T.KR[:]) for h in range(2)], 64, 256, ["KR"], ["MW"])
+        anchor = len(tasks) - 1
+        if CFG["cut"][t] < 17:
+            r_load(CFG["cut"][t], 17)
+            tasks[-1]["pre"].append((anchor, None))
+            anchor += 1
         own = T.CNT[:, 4 * t:4 * t + 1]
-        mms(7, 32, [(ps[7][:, 0:32], T.BO[:], T.PB[:], True, True)], ["BO", "PB"])
-        op("v", lambda own=own: V.tensor_reduce(own, ps[7][:, 0:32], AX.X, OP.add), 32, (), [("CNT", t)], (7,))
+        mms(7, 32, [(ps[7][:, 0:32], T.BR[:], T.PB[:], True, True)], ["BR", "PB"])
+        op("v", lambda q, own=own: V.tensor_reduce(own, ps[7][:, 0:32], AX.X, OP.add), 32, (), [("CNT", t)], (7,))
         slot = lambda r, t=t: 8 * t + (me if me < r else me - 1)
         exchange(lambda r, own=own: own, lambda r, slot=slot: T.LAND[:, slot(r):slot(r) + 1], "ae%d" % t, "le%d" % t, 0,
                  [("CNT", t)], [("LAND", t)])
-        mms(6, 128, [(ps[6][0:16, h:256:2], T.KB[:, 16 * h:16 * h + 16], ID, True, True) for h in range(2)], ["KB", "IW"])
-        act(256, T.KT[0:16, :], ps[6][0:16, 0:256], AF.Copy, (), ["KT"], (6,))
+        wave[:] = [t, 2]
+        mms(4, 128, [(ps[4][0:16, h:256:2], T.KB[:, 16 * h:16 * h + 16], ID, True, True) for h in range(2)], ["KB", "IW"])
+        cp("s", 256, T.KT[0:16, :], ps[4][0:16, 0:256], (), ["KT"], (4,))
         mms(1, 32, [(ps[1][:, 0:32], ID, T.C256[:], True, False)]
             + [(ps[1][:, 0:32], T.IW[0:16, 112 - 16 * r:240 - 16 * r], T.KT[0:16, 32 * r:32 * r + 32], False, r == 7)
                for r in range(8)], ["IW", "KT", "C256"])
-        ts(32, T.DL[:], ps[1][:, 0:32], T.PW[:, 0:1], None, OP.add, None, ["PW0"], ["DL"], (1,))
-        tt(v0 * GC, T.SUM[:, 0:v0], T.D[:, :].indirect(T.DL[:, 0:2 * NS]), T.X[:, 0:v0], OP.add,
-           blk("D", 0, 16) + ["DL", "X"], ["SUMa"])
-        tt((512 - v0) * GC, T.SUM[:, v0:512], T.D[:, :].indirect(T.DL[:, 2 * NS:32]), T.X2[:, v0:512], OP.add,
-           blk("D", 0, 16) + ["DL", "X2b"], ["SUMb"])
-        act(512, T.SUM2[:], T.SUM[:], AF.Identity, ["SUMa", "SUMb"], ["SUM2"], bias=MAGIC, scale=0.4995)
-        act(512, T.X[:], T.SUM2[:], AF.Identity, ["SUM2"], ["X"], bias=-MAGIC, scale=1.0)
-        act(512, T.SG[:], T.RF[:], AF.Sign, rng4("RF"), ["SG"], bias=-32767.5, scale=1.0)
-        cp(512, T.RI[:], T.RF[:], rng4("RF") + ["SO"], ["RI"])
-        ts(512, T.TD[:], T.RI[:], 15, None, OP.bitwise_and, None, ["RI"], ["TD"])
-        ts(512, T.TE[:], T.TD[:], 17.0, None, OP.mult, None, ["TD"], ["TE"])
-        ts(512, T.SJ[:], T.TE[:], 165, None, OP.bitwise_and, None, ["TE"], ["SJ"])
-        ts(512, T.BS[:], T.RI[:], 4, 2047, OP.logical_shift_right, OP.bitwise_and, ["RI"], ["BS"])
-        tot, land = T.TOT[:, 0:1], T.LAND[:, 8 * t:8 * t + 7]
-        op("v", lambda land=land: V.tensor_reduce(tot, land, AX.X, OP.add), 8, [("LAND", t)], ["TOT"])
-        ts(32, T.MI[:], ps[1][:, 0:32], tot, own, OP.subtract, OP.subtract, ["TOT", ("CNT", t)], ["MI"], (1,))
-        ts(32, T.MJ[:], T.MI[:], 15, None, OP.bitwise_and, None, ["MI"], ["MJ"])
-        cp(32, T.ML[:], T.MJ[:], ["MJ"], ["ML"])
-        cp(256 * GC, T.MB[:, 0:256], T.SP[:, :].indirect(T.ML[:, 0:16]), ["SP", "ML"], ["MB0"])
-        act(256 * GC, T.MB[:, 256:512], T.SP[:, :].indirect(T.ML[:, 16:32]), AF.Copy, ["SP", "ML"], ["MB1"])
-        for q, kk in (("y", "MWv"), ("s", "MWs")):
-            dma(q, [(T.MW[0:128:16, 512 * r:512 * r + 512], T.MB[16 * r:16 * r + 8, :])
-                    for r in range(8) if "ys"[r % 2] == q], 32, ["MB0", "MB1"], [kk, kk + "i"])
-        r_window_load(1, ["MWvi", "MWsi"])
-        if last:
-            dma("y", [(T.SX2[:], T.X[:])], 128, ["X", "MWvi"], ["SX2"])
-            dma("y", [(T.LX2[me], T.X[16 * me:16 * me + 16, :])], 16, ["X", "MWvi"], ["LX2o"])
-            exchange(lambda r: T.SX2[r], lambda r: T.LX2[me], "ax2", "lx2", 16, ["SX2"], ["LX2"])
-            dma("y", [(T.yx[:], T.LX2[:])], 128, ["LX2", "LX2o"], ["yx"])
-        else:
-            x_forms(CFG["xr"])
-            dma("y", [(T.DX[:, r, :], T.X[16 * r:16 * r + 16, :]) for r in range(8)], 128, ["X", "MWvi"], ["DX"])
-            x_window_load([("Z", 31)])
-
-        def gather(q, buf, name, win, wk, lst, lk, n):
-            out, src = buf[:, 1024 * n:1024 * n + 1024], win[:, :].indirect(lst[:, 64 * n:64 * n + 64])
-            R, W = wk + [(lk, n // 2)], blk(name, 2 * n, 2 * n + 2)
-            if q == "v":
-                cp(1024 * GC, out, src, R, W)
+        ts(32, T.DL[:], ps[1][:, 0:32], -1.0, pw(0), OP.mult, OP.add, [("PW", 0)], ["DL"], (1,))
+        for a, b, q in runs(who.replace("a", "v")):
+            out, src = T.Y[:, 32 * a:32 * b], T.D[:, :].indirect(T.DL[:, 2 * a:2 * b])
+            if q == "s":
+                cp("s", 0, out, src, blk("D", 0, 16) + ["DL"], [("Y", a)], gat=32 * (b - a))
             else:
-                act(1024 * GC, out, src, AF.Copy, R, W)
+                tt(0, out, src, T.X[:, 32 * a:32 * b], OP.add, blk("D", 0, 16) + ["DL", "X"], [("Y", a)], gat=32 * (b - a))
+        mms(3, 512, [(ps[3][:], ID, T.CN[:], True, False), (ps[3][:], T.IH[:], T.X[:], False, False),
+                     (ps[3][:], T.IH[:], T.Y[:], False, True)], ["IW", "IH", "CN", "X"] + blk("Y", 0, 16))
+        ts(512, T.X[:], ps[3][:], MAGIC, -MAGIC, OP.add, OP.add, (), ["X"], (3,))
+        wave[:] = [t, CFG["side"]]
+        for ha, hb in CFG["prep"]:
+            a, b = 64 * ha, 64 * hb
+            ta, tc, ka, kc = T.TA[:, a:b], T.TC[:, a:b], blk("TA", ha, hb), blk("TC", ha, hb)
+            ts(b - a, ta, ps[6][:, a:b], -2.0, 131079.5, OP.mult, OP.add, (), ka, (6,))
+            ts(b - a, tc, ta, 15, None, OP.bitwise_and, None, ka, kc)
+            ts(b - a, ta, tc, float(FOUR), None, OP.mult, None, kc, ka)
+            ts(b - a, tc, ta, SPREAD, None, OP.bitwise_and, None, ka, kc)
+            ts(b - a, ps[5][:, a:b], tc, -float(FOUR), None, OP.add, None, kc, blk("SJ", ha, hb), (5,))
+        op("s", lambda q: S.activation(ps[6][:], ps[6][:], AF.Identity, bias=MAGIC - 4096, scale=0.125), 512, (), ["BS"], (6,))
+        wave[:] = [t, 1]
+        tot, land = T.TOT[:, 0:1], T.LAND[:, 8 * t:8 * t + 7]
+        op("v", lambda q, land=land: V.tensor_reduce(tot, land, AX.X, OP.add), 8, [("LAND", t)], ["TOT"])
+        ts(8, T.MI[:], T.ONE[:], tot, own, OP.add, OP.add, ["TOT", "ONE", ("CNT", t)], ["MI"])
+        ts(8, T.MJ[:], T.MI[:], 15, None, OP.bitwise_and, None, ["MI"], ["MJ"])
+        tt(16, T.WK[:], T.MJ[:], T.GI[:], OP.mult, ["MJ", "GI"], ["WK"])
+        wave[:] = [t, 3]
+        if last:
+            dma("y", [(T.SX2[:], T.X[:])], 128, 128, ["X"], ["SX2"])
+            dma("y", [(T.LX2[me], T.X[16 * me:16 * me + 16, :])], 16, 16, ["X"], ["LX2o"])
+            exchange(lambda r: T.SX2[r], lambda r: T.LX2[me], "ax2", "lx2", 16, ["SX2"], ["LX2"])
+            dma("y", [(T.yx[:], T.LX2[:])], 128, 16, ["LX2", "LX2o"], ["yx"])
+        else:
+            x_forms(t + 1, CFG["xr2"])
+            dma("y", [(T.DX[:, r, :], T.X[16 * r:16 * r + 16, :]) for r in range(8)], 128, 128, ["X"], ["DX"])
+            dma("y", [(T.XW[16 * r:16 * r + 16, :], T.DX[:]) for r in range(8)], 1024, 128, ["DX"], XWK)
+            tasks[-1]["pre"] += [(anchor, None)]
 
-        def collect(pb, c0, k, buf, name, h):
-            mms(pb, 64, [(ps[pb][:, c0:c0 + 64], wt(k, i), buf[:, 1024 * h + i:1024 * h + 1024:16], i == 0, i == 15)
-                         for i in range(16)], blk(name, 2 * h, 2 * h + 2) + [("WT", k)])
+        def gather(buf, name, win, wk, lst, lk, n):
+            cp("vs" if name + str(n) in CFG["both"][t].split() else "s", 0, buf[:, 1024 * n:1024 * n + 1024],
+               win[:, :].indirect(lst[:, 64 * n:64 * n + 64]), wk + [(lk, n)], [(name, n)], gat=1024)
 
-        tag = "3" if last else ""
-        for n, (qa, qb) in enumerate(CFG["offs" + tag]):
-            pb, a, b = 3 + n % 2, 128 * qa, 128 * qb
-            for q in range(qa, qb):
-                for h in (2 * q, 2 * q + 1):
-                    gather(CFG["gm" + tag][h], T.D, "D", T.MW, ["MWv", "MWs"], T.FAR, "FAR", h)
-                    collect(pb, 64 * h - a, W_M, T.D, "D", h)
-            ta, tc, ka, kc = T.TA[:, a:b], T.TC[:, a:b], blk("TA", qa, qb), blk("TC", qa, qb)
-            tt(b - a, ta, ps[pb][:, 0:b - a], T.SJ[:, a:b], OP.add, ["SJ"], ka, (pb,))
-            ts(b - a, tc, ta, 165, None, OP.bitwise_and, None, ka, kc)
-            ts(b - a, ta, tc, 2176.0, None, OP.mult, None, kc, ka)
+        def collect(pb, c0, w, n, buf, name, h, wk):
+            mms(pb, 64, [(ps[pb][:, c0 + n * e:c0 + n * e + n], buf[:, 1024 * h + 128 * e:1024 * h + 128 * e + 128], w,
+                          True, True) for e in range(8)], [(name, h)] + wk)
+
+        for n, (ha, hb) in enumerate(CFG["offs"][t]):
+            pb, a, b = 1 + n % 2, 64 * ha, 64 * hb
+            for h in range(ha, hb):
+                at(h, 0)
+                gather(T.DM, "DM", T.MW, ["MW"], T.FAR, "FAR", h)
+                collect(pb, 64 * h - a, T.WK[:], 8, T.DM, "DM", h, ["WK"])
+            at(ha, 1)
+            ta, tc, tf = T.TA[:, a:b], T.TC[:, a:b], T.TF[:, a:b]
+            ka, kc, kf = blk("TA", ha, hb), blk("TC", ha, hb), blk("TF", ha, hb)
+            cp("v", b - a, ta, ps[pb][:, 0:b - a], (), ka, (pb,))
+            ts(b - a, tc, ta, 15, None, OP.bitwise_and, None, ka, kc)
+            ts(b - a, tf, tc, 1.0, float(FOUR), OP.max, OP.mult, kc, kf)
+            tt(b - a, ta, ps[5][:, a:b], tf, OP.add, kf + blk("SJ", ha, hb), ka, (5,))
+            ts(b - a, tc, ta, SPREAD, None, OP.bitwise_and, None, ka, kc)
+            ts(b - a, ta, tc, 2184.5, None, OP.mult, None, kc, ka)
             ts(b - a, tc, ta, 0x7800, None, OP.bitwise_and, None, ka, kc)
-            tt(2 * (b - a), ta, tc, T.BS[:, a:b], OP.add, kc + ["BS"], ka)
-            cp(b - a, T.OFF[:, a:b], ta, ka, blk("OFF", qa, qb))
+            tt(b - a, tf, ps[6][:, a:b], tc, OP.add, kc + ["BS"], kf, (6,))
+            ts(b - a, T.OFF[:, a:b], tf, -MAGIC, None, OP.add, None, kf, blk("OFF", ha, hb))
 
-        one = [(q, q + 1) for qa, qb in CFG["offs" + tag] for q in range(qa, qb)]
-        for n, (qa, qb) in enumerate(one if last else CFG["sel"]):
-            pb, a, b = 5 + n % 3, 128 * qa, 128 * qb
-            for q in range(qa, qb):
-                for h in (2 * q, 2 * q + 1):
-                    gather(CFG["gr" + tag][h], T.G, "G", T.RW, blk("Z", 0, 32), T.OFF, "OFF", h)
-                    collect(pb, 256 + 64 * h - a, W_DIF, T.G, "G", h)
-                    collect(pb, 64 * h - a, W_SUM, T.G, "G", h)
-            tt(b - a, T.TF[:, a:b], ps[pb][:, 256:256 + b - a], T.SG[:, a:b], OP.mult, ["SG"], blk("TF", qa, qb), (pb,))
-            tt(b - a, T.RF[:, a:b], ps[pb][:, 0:b - a], T.TF[:, a:b], OP.add, blk("TF", qa, qb), blk("RF", qa, qb), (pb,))
+        for n, (ha, hb) in enumerate(CFG["sel"][t]):
+            pb, a, b = 3 + n % 2, 64 * ha, 64 * hb
+            for h in range(ha, hb):
+                at(h, 2)
+                gather(T.G, "G", T.RW, blk("Z", 0, 34), T.OFF, "OFF", h)
+                collect(pb, 128 * h - 2 * a, T.WR[:, 16 * last:16 * last + 16], 16, T.G, "G", h, blk("WR", 0, 4))
+            at(ha, 3)
+            w = 2 * (b - a)
+            tt(b - a, T.TF[:, a:b], ps[pb][:, 1:w:2], T.SG[:, a:b], OP.mult, ["SG"], blk("TF", ha, hb), (pb,))
             if not last:
-                lists_and_digits(qa, qb, T.RF, blk("RF", qa, qb))
+                tt(b - a, ps[pb][:, 0:w:2], ps[pb][:, 0:w:2], T.TF[:, a:b], OP.add, blk("TF", ha, hb), (), (pb,))
+                lists_and_digits(ha, hb, ps[pb][:, 0:w:2], (pb,))
                 continue
-            q = qa
-            dma("y", [(T.SO4[8 * q:8 * q + 8], T.RF[:, a:b])], 64, [("RF", q)], [("SO4", q)])
-            dma("y", [(T.LO4[8 * q + me], T.RF[16 * me:16 * me + 16, a:b])], 8, [("RF", q)], [("LO4o", q)])
-            exchange(lambda r, q=q: T.SO4[8 * q + r], lambda r, q=q: T.LO4[8 * q + me], "ao%d" % q, "lo%d" % q, 8,
-                     [("SO4", q)], [("LO4", q)])
+            tt(b - a, T.RF[:, a:b], ps[pb][:, 0:w:2], T.TF[:, a:b], OP.add, blk("TF", ha, hb), blk("RF", ha, hb), (pb,))
+            for q, (oa, ob) in enumerate(CFG["out"]):
+                if ha < ob <= hb:
+                    a, b, w, R = 64 * oa, 64 * ob, ob - oa, blk("RF", oa, ob)
+                    so, lo = T["SO%d" % q], T["LO%d" % q]
+                    dma("y", [(so[:], T.RF[:, a:b]), (lo[me], T.RF[16 * me:16 * me + 16, a:b])], 36 * w, 144, R, [("SO", q)])
+                    exchange(lambda r, so=so: so[r], lambda r, lo=lo: lo[me], "ao%d" % q, "lo%d" % q, 4 * w,
+                             [("SO", q)], [("LO", q)])
+                    dma("y", [(T.yr[:, a:b], lo[:])], 32 * w, 128, [("LO", q), ("SO", q)], [("yr", q)])
         if not last:
-            r_window_store()
-    for q in range(4):
-        dma("s", [(T.yr[:, 128 * q:128 * q + 128], T.LO4[8 * q:8 * q + 8])], 64,
-            [("LO4", q), ("LO4o", q)] + blk("G", 0, 16), [("yr", q)])
+            r_forms(CFG["store"], t + 1)
 
     plans = {c: engine_plan(topo, cores, c) for c in cores}
     total, known, tok, nd, todo = {}, {q: {} for q in Q}, {}, [0], {}
@@ -437,9 +577,8 @@ def rank_program(g, core, T, topo):
                 Q[q].wait_ge(T.sem[s], v)
                 known[q][s] = v
 
-    for k in order(tasks):
+    for k, q in order(tasks, COST):
         tk = tasks[k]
-        q = tk["q"]
         wait(q, [tok[p][w] for p, w in tk["pre"] if w])
         if tk["kind"] == "op":
             s = "c" + q
@@ -448,7 +587,7 @@ def rank_program(g, core, T, topo):
                     todo[tk["acc"]] -= 1
                     ins = PE.matmul(call[0], call[1], call[2], False, todo[tk["acc"]] == 0)
                 else:
-                    ins = call()
+                    ins = call(q)
                 ins.then_inc(T.sem[s], 1)
                 total[s] = total.get(s, 0) + 1
             tok[k] = {"R": (s, total[s]), "W": (s, total[s])}

from concourse.bass import DstId, RemoteDMATransfer
from concourse.mybir import AluOpType as OP, AxisListType as AX, ActivationFunctionType as AF

RO = 3
WN = 34816
MAGIC = 12582912.0
FOUR, SPREAD = 4369, 33825
B, F, I, U = "bfloat16", "float32", "int32", "uint16"
G16 = "g" * 16
CFG = {
    "vote": ("ssssssaaaavvvvvv", "ssssaaaaaaaaaavv", "ssssaaaaaaaaaavv"),
    "fill": "vvvssddvdsgvddvdgdsgdddvdsdvvggsgg",
    "offs": (((0, 1), (1, 5), (5, 7), (7, 8)),) * 2 + (((0, 2), (2, 4), (4, 7), (7, 8)),),
    "sel": (((0, 1), (1, 5), (5, 8)),) * 2 + (((0, 2), (2, 4), (4, 6), (6, 8)),),
    "prep": ((0, 6), (6, 8)), "store": ((0, 6), (6, 8)),
    "in": ((0, 5), (5, 8)), "out": ((0, 2), (2, 4), (4, 6), (6, 8)),
    "xr": ((192, 384, "svssvsvvssvsvvvv"), (384, 512, G16)),
    "xr2": ((128, 320, G16), (320, 512, G16)),
    "both": ("DM1 DM5 G0 G1 G2 G4 G5 G6 G7",) * 2 + ("DM2 DM3 DM6 G1 G2 G4 G6",),
    "cut": (9, 16, 16),
    "xw": "vvsvvssv",
    "lead": (-10.1, -9.4, -1.2, -0.8, 14.0, 4.0), "lead3": (-3.0, -2.1, 4.0, 5.4), "swap": 1004.0, "side": 15.0,
    "hold": 1, "wait": 1, "early": 6000.0, "ahead": 3, "passes": 2, "delta": 0.2,
}
ORDER = []
COST = {"cyc": 0.83, "g": 1.56, "pe": 0.42, "dma": 900.0, "kb": 1.5, "row": 0.7, "rem": 1600.0, "link": 200.0, "call": 400.0,
        "op": -35.0, "sem": 140.0, "iss": 40.0}

SCRATCH = {
    "RW": ("sbuf", [128, WN], B), "XW": ("sbuf", [128, 4096], B), "MW": ("sbuf", [128, 4096], B),
    "D": ("sbuf", [128, 8192], B), "G": ("sbuf", [128, 8192], B), "DM": ("sbuf", [128, 8192], B),
    "XR": ("sbuf", [128, 8192], B), "RL": ("sbuf", [128, 8192], B),
    "X": ("sbuf", [128, 512], B), "XT": ("sbuf", [128, 512], B), "Y": ("sbuf", [128, 512], B),
    "ROT": ("sbuf", [128, 512], I), "R16": ("sbuf", [128, 512], U), "R16b": ("sbuf", [128, 512], U),
    "RF": ("sbuf", [128, 512], F), "FAR": ("sbuf", [128, 512], U),
    "OFF": ("sbuf", [128, 512], U), "HI": ("sbuf", [128, 512], B), "LO": ("sbuf", [128, 512], B),
    "SG": ("sbuf", [128, 512], B),
    "TA": ("sbuf", [128, 512], I), "TC": ("sbuf", [128, 512], I), "TF": ("sbuf", [128, 512], F),
    "SO": ("sbuf", [128, 512], F), "KR": ("sbuf", [128, 128], B),
    "KI": ("sbuf", [128, 32], I), "KP": ("sbuf", [128, 32], I), "KK": ("sbuf", [128, 32], I),
    "PB": ("sbuf", [128, 32], B), "KB": ("sbuf", [128, 32], B), "KT": ("sbuf", [128, 256], B),
    "DL": ("sbuf", [128, 32], U), "MI": ("sbuf", [128, 8], I), "MJ": ("sbuf", [128, 8], I),
    "CNT": ("sbuf", [128, 16], F), "LAND": ("sbuf", [128, 24], F), "TOT": ("sbuf", [128, 4], F),
    "IWv": ("sbuf", [128, 240], F), "IW": ("sbuf", [128, 240], B), "BOv": ("sbuf", [128, 128], F),
    "BOc": ("sbuf", [128, 128], F), "BO": ("sbuf", [128, 128], B), "TB": ("sbuf", [128, 512], B),
    "RM": ("sbuf", [128, 512], B), "C256": ("sbuf", [128, 32], B), "PI": ("sbuf", [128, 4], I), "PJ": ("sbuf", [128, 4], I),
    "PW": ("sbuf", [128, 12], F), "KS": ("sbuf", [128, 512], B), "KSv": ("sbuf", [128, 512], B),
    "BR": ("sbuf", [128, 128], B), "ONE": ("sbuf", [128, 8], F), "IH": ("sbuf", [128, 128], B), "CN": ("sbuf", [128, 512], B),
    "GI": ("sbuf", [128, 8], F), "SEL": ("sbuf", [128, 1024], B), "EE": ("sbuf", [128, 2048], B), "WT": ("sbuf", [128, 3 * 144], B),
    "WK": ("sbuf", [128, 8], B), "WR": ("sbuf", [128, 32], B), "IL": ("sbuf", [128, 240], B), "ER": ("sbuf", [128, 8 * 240], B),
    "SX": ("dram", [8, 128, 64], B), "LX": ("dram", [8, 128, 64], B),
    "SX2": ("dram", [8, 128, 64], B), "LX2": ("dram", [8, 128, 64], B),
    "DX": ("dram", [16, 8, 512], B), "DR": ("dram", [4, 17, 2048], B),
}
for _q, (_a, _b) in enumerate(CFG["in"]):
    SCRATCH["SR%d" % _q] = SCRATCH["LR%d" % _q] = ("dram", [8, 128, 8 * (_b - _a)], U)
for _q, (_a, _b) in enumerate(CFG["out"]):
    SCRATCH["SO%d" % _q] = SCRATCH["LO%d" % _q] = ("dram", [8, 128, 8 * (_b - _a)], F)
for _b in range(8):
    SCRATCH["ps%d" % _b] = ("psum", [128, 512], F)

SEMAPHORES = (["cv", "cs", "cp", "cg", "ax", "lx", "ax2", "lx2"]
              + [k + "r%d" % q for q in range(len(CFG["in"])) for k in "al"]
              + [k + "e%d" % t for t in range(RO) for k in "al"]
              + [k + "o%d" % q for q in range(len(CFG["out"])) for k in "al"]
              + ["d%d" % k for k in range(70)])


def engine_plan(topo, cores, src):
    off = [c for c in cores if topo.chip(c) != topo.chip(src)]
    on = [c for c in cores if c != src and topo.chip(c) == topo.chip(src)]
    eoff = topo.engines(src, off[0])
    eon = [e for e in topo.engines(src, on[0]) if e not in eoff]
    plan = {}
    for dsts, eng in ((off, eoff), (on, eon)):
        n = 1
        while 2 * n * len(dsts) <= len(eng):
            n *= 2
        for k, c in enumerate(dsts):
            plan[c] = eng[k * n:(k + 1) * n]
    return plan


def times(tk, C):
    kind, a, b, c = tk["cost"]
    if kind == "op":
        return (max(a + b * C["g"], 64) * C["cyc"] + c + C["op"], 0.0, C["sem"])
    if kind == "pe":
        return (a * C["pe"], 0.0, 60.0 + C["sem"])
    if kind == "dma":
        return (C["iss"] * a, b * C["kb"] + c * C["row"], C["dma"])
    return (C["call"], C["link"] * a, C["rem"])


def place(tm, before, rank):
    n = len(tm)
    after = [[] for _ in range(n)]
    left = [len(before[k]) for k in range(n)]
    for k in range(n):
        for p, _gap in before[k]:
            after[p].append(k)
    ready = [k for k in range(n) if left[k] == 0]
    start, busy = [0.0] * n, {}
    while ready:
        k = min(ready, key=lambda j: rank[j])
        ready.remove(k)
        s, moved = max([start[p] + gap for p, gap in before[k]], default=0.0), True
        while moved:
            moved = False
            for q, off, d in tm[k]:
                for a, b in busy.get(q, ()):
                    if a < s + off + d and s + off < b:
                        s, moved = b - off, True
        start[k] = s
        for q, off, d in tm[k]:
            busy.setdefault(q, []).append((s + off, s + off + d))
        for j in after[k]:
            left[j] -= 1
            if left[j] == 0:
                ready.append(j)
    return start


def forward(tasks, tm, rank):
    n = len(tasks)
    succ = [set() for _ in range(n)]
    for k, t in enumerate(tasks):
        for p, _w in t["pre"]:
            succ[p].add(k)
    left = [len(set(p for p, _w in t["pre"])) for t in tasks]
    est, free, out = {k: 0.0 for k in range(n) if left[k] == 0}, {}, []
    fin, end = [0.0] * n, [0.0] * n
    while est:
        t0, q = min((max(e, free.get(x, 0.0)), x) for k, e in est.items() for x in tasks[k]["q"])
        mine = sorted((rank[k], k) for k in est if q in tasks[k]["q"])
        now = [k for _r, k in mine if est[k] <= t0][0]
        k = [j for _r, j in mine if est[j] <= t0 + CFG["delta"] * tm[now][0]][0]
        end[k] = free[q] = max(est.pop(k), free.get(q, 0.0)) + tm[k][0]
        fin[k] = end[k] + tm[k][2]
        if tm[k][1]:
            free["engines"] = max(free.get("engines", 0.0), end[k]) + tm[k][1]
            fin[k] = free["engines"] + tm[k][2]
        out.append((k, q))
        for s in succ[k]:
            left[s] -= 1
            if left[s] == 0:
                est[s] = max(fin[p] if w else end[p] for p, w in tasks[s]["pre"])
    return out, fin


def order(tasks, C):
    if ORDER:
        return ORDER
    n = len(tasks)
    tm = [times(t, C) for t in tasks]
    whole = [sum(x) + t.get("early", 0.0) for t, x in zip(tasks, tm)]
    pre, post = [{} for _ in range(n)], [{} for _ in range(n)]
    for k, t in enumerate(tasks):
        for p, w in t["pre"]:
            pre[k][p] = max(pre[k].get(p, 0.0), whole[p] if w else tm[p][0])
    for k in range(n):
        for p, gap in pre[k].items():
            post[p][k] = whole[k] - whole[p] + gap
    post = [list(d.items()) for d in post]
    back, best = place([()] * n, post, range(n)), None
    for _ in range(CFG["passes"]):
        rank = [-(back[k] + whole[k]) for k in range(n)]
        for k, t in enumerate(tasks):
            if "wave" in t:
                rank[k] = 1000.0 * t["wave"][0] + t["wave"][1] + 1e-4 * k
        out, fin = forward(tasks, tm, rank)
        if best is None or max(fin) < best[0]:
            best = (max(fin), out)
        bw = [None] * n
        for k, q in out:
            bw[k] = [(q, whole[k] - tm[k][0], tm[k][0])]
            if tm[k][1]:
                bw[k].append(("engines", whole[k] - tm[k][0] - tm[k][1], tm[k][1]))
        back = place(bw, post, [-x for x in fin])
    ORDER.extend(best[1])
    return ORDER


def rank_program(g, core, T, topo):
    me = T.rank_of(core)
    if me is None:
        return
    cores = list(T.cores)
    Q = {"v": g.vector, "s": g.scalar, "p": g.tensor, "y": g.sync, "g": g}
    tasks, writer, readers, bank, base, wave = [], {}, {}, {}, {}, []

    def task(q, kind, body, cost, R=(), W=(), P=(), acc=None):
        k = len(tasks)
        pre = [(writer[x], "W") for x in R if x in writer]
        for x in W:
            if x in writer:
                pre.append((writer[x], "W"))
            pre += [(p, "R") for p in readers.get(x, [])]
        for b in P:
            if acc is not None and acc not in base:
                base[acc] = list(bank.get(b, []))
                bank[b] = []
            pre += [(p, None if tasks[p]["q"] == q == "p" else "W") for p in (base[acc] if acc is not None else bank.get(b, []))]
            bank[b] = (bank[b] if acc is not None else []) + [k]
        tasks.append({"q": q, "kind": kind, "body": body, "cost": cost, "pre": pre, "acc": acc,
                      "name": (list(W) + list(P) + ["-"])[0]})
        if wave:
            tasks[-1]["wave"] = tuple(wave)
        for x in R:
            readers.setdefault(x, []).append(k)
        for x in W:
            writer[x] = k
            readers[x] = []

    def op(q, call, d, R=(), W=(), P=(), gat=0):
        task(q, "op", [call], ("op", d, gat, 150 if q == "g" else 60 if d + gat > 64 else 20), R, W, P)

    def dma(q, moves, kb, rows, R=(), W=(), early=0.0):
        task(q, "dma", moves, ("dma", len(moves), kb, rows), R, W)
        tasks[-1]["early"] = early

    def exchange(src_of, dst_of, sa, sl, kb, R, W):
        task("g", "rem", (src_of, dst_of, sa, sl), ("rem", kb, 0, 0), R, W)

    V, S, PE = g.vector, g.scalar, g.tensor
    ps = [T["ps%d" % b] for b in range(8)]
    ID = T.IW[:, 112:240]
    blk = lambda n, a, b: [(n, c) for c in range(a, b)]
    all8 = lambda n: blk(n, 0, 8)

    def ts(d, out, in0, a, b, o0, o1=None, R=(), W=(), P=()):
        if o1 is None:
            op("v", lambda q: V.tensor_scalar(out, in0, a, None, o0), d, R, W, P)
        else:
            op("v", lambda q: V.tensor_scalar(out, in0, a, b, o0, o1), d, R, W, P)

    def tt(d, out, in0, in1, o, R=(), W=(), P=(), gat=0):
        op("v", lambda q: V.tensor_tensor(out, in0, in1, o), d, R, W, P, gat)

    def cp(who, d, out, in_, R=(), W=(), P=(), gat=0):
        op(who, lambda q: V.tensor_copy(out, in_) if q == "v" else S.activation(out, in_, AF.Copy), d, R, W, P, gat)

    def mms(b, n, lst, R, acc=None):
        task("p", "op", [(lambda q, a=a: PE.matmul(*a)) for a in lst] if acc is None else lst,
             ("pe", max(n, 64) * len(lst), 0, 0), R, (), (b,), acc)

    def iota(d, out, pattern, base_, cm, W, R=()):
        op("g", lambda q: g.iota(out, pattern, base_, cm, allow_small_or_imprecise_dtypes=True), 2 * d, R, W)

    wt = lambda k, c: T.WT[:, 144 * k + 15 - c:144 * k + 143 - c]
    W_RELU, W_NEG, W_ABS = range(3)

    dma("y", [(T.SX[:], T.x[:])], 128, 16, (), ["SX"])
    for h, (ha, hb) in enumerate(CFG["in"]):
        dma("s", [(T.ROT[:, 64 * ha:64 * hb], T.rot[:, 64 * ha:64 * hb])], 32 * (hb - ha), 128, (), [("ROT", h)])
    dma("y", [(T.LX[me], T.x[16 * me:16 * me + 16, :])], 16, 16, (), ["LXo"])
    iota(240, T.IWv[:], [[1, 240]], -112, -1, ["IWv"])
    iota(128, T.BOv[:], [[-16, 8], [0, 16]], 0, 1, ["BOv"])
    op("g", lambda q: g.iota(T.PI[:, 0:1], [[0, 1]], 0, 1), 1, (), ["PI"])
    iota(32, T.C256[:], [[-256, 32]], 0, 0, ["C256"])
    iota(512, T.KSv[:], [[1, 4], [0, 4], [4, 32]], 0, -1, ["KSv"])
    iota(512, T.TB[:], [[0, 32], [-1, 16]], 15, 0, ["TB"])
    for h, (ha, hb) in enumerate(CFG["in"]):
        cp("v", 64 * (hb - ha), T.R16[:, 64 * ha:64 * hb], T.ROT[:, 64 * ha:64 * hb], [("ROT", h)], [("R16", h)])
    exchange(lambda r: T.SX[r], lambda r: T.LX[me], "ax", "lx", 16, ["SX"] + blk("R16", 0, CFG["hold"]), ["LX"])
    sent = len(tasks) - 1
    dma("y", [(T.X[:], T.LX[:])], 128, 128, ["LX", "LXo"], ["X"])
    for h, (ha, hb) in enumerate(CFG["in"]):
        a, b, w, sr, lr = 64 * ha, 64 * hb, hb - ha, T["SR%d" % h], T["LR%d" % h]
        dma("y", [(sr[:], T.R16[:, a:b]), (lr[me], T.R16[16 * me:16 * me + 16, a:b])], 18 * w, 144, [("R16", h)], [("SR", h)])
        exchange(lambda r, sr=sr: sr[r], lambda r, lr=lr: lr[me], "ar%d" % h, "lr%d" % h, 2 * w,
                 [("SR", h)] + ["LX"] * (h > 0 and CFG["wait"]), [("LR", h)])
        tasks[-1]["pre"].append((sent, None))
        dma("y", [(T.R16b[:, a:b], lr[:])], 16 * w, 128, [("LR", h), ("SR", h)], [("R16b", h)])
    LAST = ("R16b", len(CFG["in"]) - 1)
    k = 0
    while k < 34:
        q, n = CFG["fill"][k], 1
        while q != "s" and k + n < 34 and CFG["fill"][k + n] == q and n < 2:
            n += 1
        w = T.RW[:, 1024 * k:1024 * (k + n)]
        if q == "d":
            dma("y", [(w, T.RW[:, 0:1024 * n])], 256 * n, 128, blk("Z", 0, n) + [LAST], blk("Z", k, k + n))
        elif q == "v":
            op("v", lambda q, w=w: V.memset(w, 1.0), 512 * n, (), blk("Z", k, k + n))
        elif q == "s":
            cp("s", 1024, w, T.RW[:, 0:1024], [("Z", 0)], [("Z", k)])
        else:
            iota(1024 * n, w, [[0, 1024 * n]], 1, 0, blk("Z", k, k + n), [("SR", 0)])
        k += n
    op("v", lambda q: V.memset(T.MW[:], 0.0), 2048, (), ["MW"])
    dma("y", [(T.MW[1 + r:128:16, 512 * r:512 * r + 512], T.RW[0:8, 0:512]) for r in range(8)], 64, 64, [("Z", 0), LAST], ["MW"])
    dma("y", [(T.DR[0:2, 16, :], T.RW[0:4, 0:1024]), (T.DR[2:4, 0, :], T.RW[0:4, 0:1024])], 16, 8, [("Z", 0)], ["DR0"])

    ts(240, T.IW[:], T.IWv[:], 0.0, None, OP.is_equal, None, ["IWv"], ["IW"])
    ts(128, T.BOc[:], T.BOv[:], 0.0, 15.0, OP.max, OP.min, ["BOv"], ["BOc"])
    op("v", lambda q: V.memset(T.WT[:], 0.0), 216, (), ["WT0"])
    op("v", lambda q: V.memset(T.CN[:], -15.0 / 64), 256, (), ["CN"])
    ts(1, T.PJ[:, 0:1], T.PI[:, 0:1], 15, None, OP.bitwise_and, None, ["PI"], ["PJ"])
    ts(256, T.RM[:], T.TB[:], 15.0, None, OP.not_equal, None, ["TB"], ["RM"])
    tt(256, T.BO[:], T.BOc[:], T.BOv[:], OP.is_equal, ["BOc", "BOv"], ["BO"])
    ts(64, T.IH[:], ID, 0.5, None, OP.mult, None, ["IW"], ["IH"])
    place_ = T.PJ[:, 0:1]
    pw = lambda k: T.PW[:, k:k + 1]
    ts(1, pw(0), place_, 16.0, 15.0, OP.mult, OP.add, ["PJ"], [("PW", 0)])
    ts(1, pw(2), place_, 2.0, None, OP.is_lt, None, ["PJ"], [("PW", 2)])
    ts(1, pw(3), place_, 4.0, -0.5, OP.is_lt, OP.mult, ["PJ"], [("PW", 3)])
    ts(1, pw(4), pw(3), pw(2), 2.0 ** -13, OP.add, OP.mult, [("PW", 2), ("PW", 3)], [("PW", 4)])
    ts(1, pw(5), place_, -1.0, 15.0, OP.mult, OP.add, ["PJ"], [("PW", 5)])
    ts(1, pw(6), T.PI[:, 0:1], pw(5), -15.0, OP.add, OP.add, ["PI", ("PW", 5)], [("PW", 6)])
    ts(1, pw(7), place_, 4.0, -32768.0, OP.is_equal, OP.mult, ["PJ"], [("PW", 7)])
    ts(1, pw(8), pw(7), pw(2), 2.0, OP.add, OP.mult, [("PW", 2), ("PW", 7)], [("PW", 8)])
    ts(1, pw(9), pw(4), 2.0, None, OP.mult, None, [("PW", 4)], [("PW", 9)])
    ts(1, pw(1), pw(6), -0.0625, 14.0, OP.mult, OP.add, [("PW", 6)], [("PW", 1)])
    GC8 = T.BO[:, 0:128:16]
    for k, w in enumerate((32.0, -16.0, 16.0)):
        ts(8, T.WT[:, 144 * k + 15:144 * k + 143:16], GC8, w, None, OP.mult, None, ["BO", "WT0"], [("WT", k)])
    ts(64, T.BR[:], T.TB[:, 0:128], pw(1), None, OP.is_equal, None, ["TB", ("PW", 1)], ["BR"])
    ts(256, T.KS[:], T.KSv[:], 0.0, None, OP.is_equal, None, ["KSv"], ["KS"])
    op("v", lambda q: V.memset(T.ONE[:], 1.0), 8, (), ["ONE"])
    for k, w in enumerate((2, 4, 8, 9)):
        a = 16 * (k // 2) + k % 2
        ts(8, T.WR[:, a:a + 15:2], GC8, pw(w), None, OP.mult, None, ["BO", ("PW", w)], [("WR", k)])
    for i in range(16):
        ts(64, T.EE[:, i:2048:16], ID, -1.0, None, OP.mult, None, ["IW"], [("EE", i)])

    XWK = blk("XW", 0, 8)
    cp("v", 8, T.GI[:], GC8, ["BO"], ["GI"])
    for r in range(8):
        sel = T.SEL[:, 128 * r:128 * r + 128]
        ts(64, sel, T.TB[:, 0:128], pw(5), T.GI[:, r:r + 1], OP.is_equal, OP.mult, ["TB", ("PW", 5), "GI"], [("SEL", r)])
        b = (0, 1, 2, 3, 4, 6, 1, 0)[r]
        mms(b, 512, [(ps[b][:], sel, T.X[:], True, True)], [("SEL", r), "X"])
        cp(CFG["xw"][r], 512, T.XW[:, 512 * r:512 * r + 512], ps[b][:], (), [("XW", r)], (b,))
    ts(240, T.IL[:], T.IWv[:], pw(6), 0.0, OP.add, OP.is_equal, ["IWv", ("PW", 6)], ["IL"])
    for r in range(8):
        ts(120, T.ER[:, 240 * r:240 * r + 240], T.IL[:], T.GI[:, r:r + 1], None, OP.mult, None, ["IL", "GI"], [("ER", r)])

    def runs(s):
        cut = [k for k in range(len(s)) if k == 0 or s[k] != s[k - 1]] + [len(s)]
        return [(a, b, s[a]) for a, b in zip(cut, cut[1:])]

    def x_forms(t, jobs):
        vbs = sorted(set(c // 4 for c in range(16) if CFG["vote"][t][c] == "s"))
        mms(7, 128, [(ps[7][:, 128 * vb:128 * vb + 128], T.X[:, 128 * vb:128 * vb + 128], ID, True, True)
                     for vb in vbs], ["X", "IW"])
        a, b = 128 * vbs[0], 128 * vbs[-1] + 128
        cp("s", b - a, T.XT[:, a:b], ps[7][:, a:b], (), ["XT"], (7,))
        for a, b, who in jobs:
            for i in range(16):
                out, in_, W = T.XR[:, 16 * a + i:16 * b:16], T.X[:, a:b], [("XR", c, i) for c in range(a // 32, b // 32)]
                if who[i] == "g":
                    op("g", lambda q, out=out, in_=in_, n=b - a: g.affine_select(out, in_, [[0, n]], OP.is_ge, 0.0, 0, 0),
                       2 * (b - a), ["X"], W)
                else:
                    cp(who[i], (b - a) // (2 if who[i] == "v" else 1), out, in_, ["X"], W)

    def lists_and_digits(ha, hb, src, P):
        a, b = 64 * ha, 64 * hb
        ts(b - a, T.FAR[:, a:b], src, 0.125, -4096.46875, OP.mult, OP.add, (), blk("FAR", ha, hb), P)
        wave[1] += CFG["lead"][5]
        cp("s", b - a, T.HI[:, a:b], src, (), blk("HI", ha, hb), P)
        tt(b - a, T.LO[:, a:b], src, T.HI[:, a:b], OP.subtract, blk("HI", ha, hb), blk("LO", ha, hb), P)

    def r_load(a, b):
        dma("y", [(T.RW[16 * r:16 * r + 4, 2048 * a:2048 * b], T.DR[:, a:b, :]) for r in range(8)], 128 * (b - a), 128,
            all8("DR") + ["DR0"], blk("Z", 2 * a, 2 * b), CFG["early"])

    def r_forms(parts, t):
        for ha, hb in parts:
            a, b = 64 * ha, 64 * hb
            dma("y", [(T.DR[2 * (r // 4) + d, r // 4:16 + r // 4, 512 * (r % 4) + a:512 * (r % 4) + b],
                       buf[16 * r:16 * r + 16, a:b])
                      for d, buf in enumerate((T.HI, T.LO)) for r in range(8)], 32 * (hb - ha), 256,
                blk("HI", ha, hb) + blk("LO", ha, hb), blk("DR", ha, hb))
        r_load(0, CFG["cut"][t])
        wave[:] = [t - 1, CFG["swap"]]
        ts(256, T.SG[:], T.FAR[:], 2048.0, -16384.0, OP.is_ge, OP.mult, all8("FAR"), ["SG"])
        er = lambda r, c: T.ER[:, 240 * r + 112 - 16 * c:240 * r + 240 - 16 * c]
        for r in range(8):
            for d, buf in enumerate((T.HI, T.LO)):
                mms(6, 64, [(ps[6][:, r:512:8], T.BO[:], T.CN[:, 0:64], True, False)][d:]
                    + [(ps[6][:, r:512:8], er(r, c), buf[:, c:512:8], False, d == 1 and c == 7) for c in range(8)],
                    all8("HI") + all8("LO") + ["BO", "CN", ("ER", r)])

    x_forms(0, CFG["xr"])
    for h, (ha, hb) in enumerate(CFG["in"]):
        a, b, R = 64 * ha, 64 * hb, [("R16b", h)]
        ts((b - a) // 2, T.FAR[:, a:b], T.R16b[:, a:b], 0.0625, -0.46875, OP.mult, OP.add, R, blk("FAR", ha, hb))
        ts(b - a, ps[5][:, a:b], T.R16b[:, a:b], 0.5, 32768.0, OP.mult, OP.add, R, (), (5,))
        cp("s", b - a, T.HI[:, a:b], ps[5][:, a:b], (), blk("HI", ha, hb), (5,))
        tt(b - a, T.LO[:, a:b], ps[5][:, a:b], T.HI[:, a:b], OP.subtract, blk("HI", ha, hb), blk("LO", ha, hb), (5,))
    r_forms(((0, 8),), 0)
    wave[:] = []

    for t in range(RO):
        def at(h, stage, t=t):
            lead = CFG["lead3" if t == RO - 1 and stage < 4 else "lead"]
            wave[:] = [] if t == 0 and stage == 4 else [t - (stage == 4), 20 + h + lead[stage]]

        last = t == RO - 1
        who = CFG["vote"][t]
        EEK, acc = blk("EE", 0, 16), "key%d" % t
        mms(0, 512, [(ps[0][:], ID, T.TB[:], True, False)], ["IW", "TB"])

        def key(k, c, buf, name):
            mms(0, 512, [(ps[0][:], wt(k, c), buf[:, 512 * c:512 * c + 512])], [(name, c), ("WT", k)], acc)

        sb = (1, 2, 3, 4) if t == 0 else (1, 2)
        done = []
        for n, c in enumerate(c for c in range(16) if who[c] == "s"):
            at(c / 2, 4)
            b = sb[n % len(sb)]
            mms(b, 512, [(ps[b][:], T.XT[:, 128 * (c // 4):128 * (c // 4) + 128],
                          T.EE[:, 512 * (c % 4):512 * (c % 4) + 512], True, False)], ["XT"] + EEK)
            cp("s", 0, T.D[:, 512 * c:512 * c + 512], T.XW[:, :].indirect(T.FAR[:, 32 * c:32 * c + 32]),
               XWK + [("FAR", c // 2)], [("D", c)], gat=512)
            if n >= CFG["ahead"]:
                tasks[-1]["pre"].append((done[n - CFG["ahead"]], None))
            mms(b, 512, [(ps[b][:], ID, T.D[:, 512 * c:512 * c + 512], False, True)], ["IW", ("D", c)])
            op("s", lambda q, c=c, b=b: S.activation(T.RL[:, 512 * c:512 * c + 512], ps[b][:], AF.Abs), 512, (), [("RL", c)], (b,))
            done.append(len(tasks) - 1)
            key(W_ABS, c, T.RL, "RL")
        done = []
        vs = [c for c in range(16) if who[c] != "s"]
        while vs:
            a = vs[0]
            b = a + 2 if len(vs) > 3 and a % 2 == 0 and who[a + 1] == who[a] else a + 1
            vs = vs[b - a:]
            at(a / 2, 4)
            tt(0, T.D[:, 512 * a:512 * b], T.XW[:, :].indirect(T.FAR[:, 32 * a:32 * b]),
               T.XR[:, 512 * a:512 * b], OP.subtract,
               XWK + [("FAR", a // 2)] + [("XR", c, i) for c in range(a, b) for i in range(16)], blk("D", a, b), gat=512 * (b - a))
            if len(done) >= 2:
                tasks[-1]["pre"].append((done[-2], None))
            if who[a] == "a":
                for c in range(a, b):
                    op("s", lambda q, c=c: S.activation(T.RL[:, 512 * c:512 * c + 512], T.D[:, 512 * c:512 * c + 512], AF.Abs),
                       512, [("D", c)], [("RL", c)])
                    key(W_ABS, c, T.RL, "RL")
                continue
            ts(256 * (b - a), T.RL[:, 512 * a:512 * b], T.D[:, 512 * a:512 * b], 0.0, None, OP.max, None,
               blk("D", a, b), blk("RL", a, b))
            done.append(len(tasks) - 1)
            for c in range(a, b):
                key(W_NEG, c, T.D, "D")
                key(W_RELU, c, T.RL, "RL")
        wave[:] = [t, 0]
        op("v", lambda q: V.tensor_tensor_scan(T.SO[:], T.RM[:], ps[0][:], 0.0, OP.mult, OP.max), 512, ["RM"], ["SO"], (0,))
        cp("v", 32, T.KI[:], T.SO[:, 15:512:16], ["SO"], ["KI"])
        ts(32, T.KK[:], T.KI[:], 15, None, OP.bitwise_and, None, ["KI"], ["KK"])
        ts(32, T.KP[:], T.KI[:], 1, None, OP.bitwise_and, None, ["KI"], ["KP"])
        cp("v", 32, T.KB[:], T.KK[:], ["KK"], ["KB"])
        cp("v", 32, T.PB[:], T.KP[:], ["KP"], ["PB"])
        mms(2, 32, [(ps[2][:, 32 * c:32 * c + 32], T.KS[:, 128 * c:128 * c + 128], T.KB[:], True, True) for c in range(4)],
            ["KS", "KB"])
        cp("s", 128, T.KR[:], ps[2][:, 0:128], (), ["KR"], (2,))
        dma("y", [(T.MW[64 * h:64 * h + 64:16, :], T.KR[:]) for h in range(2)], 64, 256, ["KR"], ["MW"])
        anchor = len(tasks) - 1
        if CFG["cut"][t] < 17:
            r_load(CFG["cut"][t], 17)
            tasks[-1]["pre"].append((anchor, None))
            anchor += 1
        own = T.CNT[:, 4 * t:4 * t + 1]
        mms(7, 32, [(ps[7][:, 0:32], T.BR[:], T.PB[:], True, True)], ["BR", "PB"])
        op("v", lambda q, own=own: V.tensor_reduce(own, ps[7][:, 0:32], AX.X, OP.add), 32, (), [("CNT", t)], (7,))
        slot = lambda r, t=t: 8 * t + (me if me < r else me - 1)
        exchange(lambda r, own=own: own, lambda r, slot=slot: T.LAND[:, slot(r):slot(r) + 1], "ae%d" % t, "le%d" % t, 0,
                 [("CNT", t)], [("LAND", t)])
        wave[:] = [t, 2]
        mms(4, 128, [(ps[4][0:16, h:256:2], T.KB[:, 16 * h:16 * h + 16], ID, True, True) for h in range(2)], ["KB", "IW"])
        cp("s", 256, T.KT[0:16, :], ps[4][0:16, 0:256], (), ["KT"], (4,))
        mms(1, 32, [(ps[1][:, 0:32], ID, T.C256[:], True, False)]
            + [(ps[1][:, 0:32], T.IW[0:16, 112 - 16 * r:240 - 16 * r], T.KT[0:16, 32 * r:32 * r + 32], False, r == 7)
               for r in range(8)], ["IW", "KT", "C256"])
        ts(32, T.DL[:], ps[1][:, 0:32], -1.0, pw(0), OP.mult, OP.add, [("PW", 0)], ["DL"], (1,))
        for a, b, q in runs(who.replace("a", "v")):
            out, src = T.Y[:, 32 * a:32 * b], T.D[:, :].indirect(T.DL[:, 2 * a:2 * b])
            if q == "s":
                cp("s", 0, out, src, blk("D", 0, 16) + ["DL"], [("Y", a)], gat=32 * (b - a))
            else:
                tt(0, out, src, T.X[:, 32 * a:32 * b], OP.add, blk("D", 0, 16) + ["DL", "X"], [("Y", a)], gat=32 * (b - a))
        mms(3, 512, [(ps[3][:], ID, T.CN[:], True, False), (ps[3][:], T.IH[:], T.X[:], False, False),
                     (ps[3][:], T.IH[:], T.Y[:], False, True)], ["IW", "IH", "CN", "X"] + blk("Y", 0, 16))
        ts(512, T.X[:], ps[3][:], MAGIC, -MAGIC, OP.add, OP.add, (), ["X"], (3,))
        wave[:] = [t, CFG["side"]]
        for ha, hb in CFG["prep"]:
            a, b = 64 * ha, 64 * hb
            ta, tc, ka, kc = T.TA[:, a:b], T.TC[:, a:b], blk("TA", ha, hb), blk("TC", ha, hb)
            ts(b - a, ta, ps[6][:, a:b], -2.0, 131079.5, OP.mult, OP.add, (), ka, (6,))
            ts(b - a, tc, ta, 15, None, OP.bitwise_and, None, ka, kc)
            ts(b - a, ta, tc, float(FOUR), None, OP.mult, None, kc, ka)
            ts(b - a, tc, ta, SPREAD, None, OP.bitwise_and, None, ka, kc)
            ts(b - a, ps[5][:, a:b], tc, -float(FOUR), None, OP.add, None, kc, blk("SJ", ha, hb), (5,))
        op("s", lambda q: S.activation(ps[6][:], ps[6][:], AF.Identity, bias=MAGIC - 4096, scale=0.125), 512, (), ["BS"], (6,))
        wave[:] = [t, 1]
        tot, land = T.TOT[:, 0:1], T.LAND[:, 8 * t:8 * t + 7]
        op("v", lambda q, land=land: V.tensor_reduce(tot, land, AX.X, OP.add), 8, [("LAND", t)], ["TOT"])
        ts(8, T.MI[:], T.ONE[:], tot, own, OP.add, OP.add, ["TOT", "ONE", ("CNT", t)], ["MI"])
        ts(8, T.MJ[:], T.MI[:], 15, None, OP.bitwise_and, None, ["MI"], ["MJ"])
        tt(16, T.WK[:], T.MJ[:], T.GI[:], OP.mult, ["MJ", "GI"], ["WK"])
        wave[:] = [t, 3]
        if last:
            dma("y", [(T.SX2[:], T.X[:])], 128, 128, ["X"], ["SX2"])
            dma("y", [(T.LX2[me], T.X[16 * me:16 * me + 16, :])], 16, 16, ["X"], ["LX2o"])
            exchange(lambda r: T.SX2[r], lambda r: T.LX2[me], "ax2", "lx2", 16, ["SX2"], ["LX2"])
            dma("y", [(T.yx[:], T.LX2[:])], 128, 16, ["LX2", "LX2o"], ["yx"])
        else:
            x_forms(t + 1, CFG["xr2"])
            dma("y", [(T.DX[:, r, :], T.X[16 * r:16 * r + 16, :]) for r in range(8)], 128, 128, ["X"], ["DX"])
            dma("y", [(T.XW[16 * r:16 * r + 16, :], T.DX[:]) for r in range(8)], 1024, 128, ["DX"], XWK)
            tasks[-1]["pre"] += [(anchor, None)]

        def gather(buf, name, win, wk, lst, lk, n):
            cp("vs" if name + str(n) in CFG["both"][t].split() else "s", 0, buf[:, 1024 * n:1024 * n + 1024],
               win[:, :].indirect(lst[:, 64 * n:64 * n + 64]), wk + [(lk, n)], [(name, n)], gat=1024)

        def collect(pb, c0, w, n, buf, name, h, wk):
            mms(pb, 64, [(ps[pb][:, c0 + n * e:c0 + n * e + n], buf[:, 1024 * h + 128 * e:1024 * h + 128 * e + 128], w,
                          True, True) for e in range(8)], [(name, h)] + wk)

        for n, (ha, hb) in enumerate(CFG["offs"][t]):
            pb, a, b = 1 + n % 2, 64 * ha, 64 * hb
            for h in range(ha, hb):
                at(h, 0)
                gather(T.DM, "DM", T.MW, ["MW"], T.FAR, "FAR", h)
                collect(pb, 64 * h - a, T.WK[:], 8, T.DM, "DM", h, ["WK"])
            at(ha, 1)
            ta, tc, tf = T.TA[:, a:b], T.TC[:, a:b], T.TF[:, a:b]
            ka, kc, kf = blk("TA", ha, hb), blk("TC", ha, hb), blk("TF", ha, hb)
            cp("v", b - a, ta, ps[pb][:, 0:b - a], (), ka, (pb,))
            ts(b - a, tc, ta, 15, None, OP.bitwise_and, None, ka, kc)
            ts(b - a, tf, tc, 1.0, float(FOUR), OP.max, OP.mult, kc, kf)
            tt(b - a, ta, ps[5][:, a:b], tf, OP.add, kf + blk("SJ", ha, hb), ka, (5,))
            ts(b - a, tc, ta, SPREAD, None, OP.bitwise_and, None, ka, kc)
            ts(b - a, ta, tc, 2184.5, None, OP.mult, None, kc, ka)
            ts(b - a, tc, ta, 0x7800, None, OP.bitwise_and, None, ka, kc)
            tt(b - a, tf, ps[6][:, a:b], tc, OP.add, kc + ["BS"], kf, (6,))
            ts(b - a, T.OFF[:, a:b], tf, -MAGIC, None, OP.add, None, kf, blk("OFF", ha, hb))

        for n, (ha, hb) in enumerate(CFG["sel"][t]):
            pb, a, b = 3 + n % 2, 64 * ha, 64 * hb
            for h in range(ha, hb):
                at(h, 2)
                gather(T.G, "G", T.RW, blk("Z", 0, 34), T.OFF, "OFF", h)
                collect(pb, 128 * h - 2 * a, T.WR[:, 16 * last:16 * last + 16], 16, T.G, "G", h, blk("WR", 0, 4))
            at(ha, 3)
            w = 2 * (b - a)
            tt(b - a, T.TF[:, a:b], ps[pb][:, 1:w:2], T.SG[:, a:b], OP.mult, ["SG"], blk("TF", ha, hb), (pb,))
            if not last:
                tt(b - a, ps[pb][:, 0:w:2], ps[pb][:, 0:w:2], T.TF[:, a:b], OP.add, blk("TF", ha, hb), (), (pb,))
                lists_and_digits(ha, hb, ps[pb][:, 0:w:2], (pb,))
                continue
            tt(b - a, T.RF[:, a:b], ps[pb][:, 0:w:2], T.TF[:, a:b], OP.add, blk("TF", ha, hb), blk("RF", ha, hb), (pb,))
            for q, (oa, ob) in enumerate(CFG["out"]):
                if ha < ob <= hb:
                    a, b, w, R = 64 * oa, 64 * ob, ob - oa, blk("RF", oa, ob)
                    so, lo = T["SO%d" % q], T["LO%d" % q]
                    dma("y", [(so[:], T.RF[:, a:b]), (lo[me], T.RF[16 * me:16 * me + 16, a:b])], 36 * w, 144, R, [("SO", q)])
                    exchange(lambda r, so=so: so[r], lambda r, lo=lo: lo[me], "ao%d" % q, "lo%d" % q, 4 * w,
                             [("SO", q)], [("LO", q)])
                    dma("y", [(T.yr[:, a:b], lo[:])], 32 * w, 128, [("LO", q), ("SO", q)], [("yr", q)])
        if not last:
            r_forms(CFG["store"], t + 1)

    plans = {c: engine_plan(topo, cores, c) for c in cores}
    total, known, tok, nd, todo = {}, {q: {} for q in Q}, {}, [0], {}
    for tk in tasks:
        todo[tk["acc"]] = todo.get(tk["acc"], 0) + 1

    def wait(q, toks):
        need = {}
        for s, v in toks:
            need[s] = max(need.get(s, 0), v)
        for s, v in need.items():
            if known[q].get(s, 0) < v:
                Q[q].wait_ge(T.sem[s], v)
                known[q][s] = v

    for k, q in order(tasks, COST):
        tk = tasks[k]
        wait(q, [tok[p][w] for p, w in tk["pre"] if w])
        if tk["kind"] == "op":
            s = "c" + q
            for call in tk["body"]:
                if tk["acc"] is not None:
                    todo[tk["acc"]] -= 1
                    ins = PE.matmul(call[0], call[1], call[2], False, todo[tk["acc"]] == 0)
                else:
                    ins = call(q)
                ins.then_inc(T.sem[s], 1)
                total[s] = total.get(s, 0) + 1
            tok[k] = {"R": (s, total[s]), "W": (s, total[s])}
        elif tk["kind"] == "dma":
            s = "d%d" % nd[0]
            nd[0] += 1
            for out, in_ in tk["body"]:
                Q[q].dma_start(out, in_).then_inc(T.sem[s], 16)
            total[s] = 16 * len(tk["body"])
            tok[k] = {"R": (s, total[s]), "W": (s, total[s])}
        else:
            src_of, dst_of, sa, sl = tk["body"]
            trs = []
            for c, eng in plans[core].items():
                rid, pid, _e = topo.addr(c)
                r = cores.index(c)
                trs.append(RemoteDMATransfer(dst_ids=[DstId(rid=rid, pnc=pid)], dma_engine_mask=sum(1 << e for e in eng),
                                             remote_sem=T.sem[sa], src=src_of(r), dst=dst_of(r)))
            g.remote_dma_fused(trs, local_sem=T.sem[sl])
            total[sl] = sum(len(e) for e in plans[core].values())
            total[sa] = sum(len(plans[c][core]) for c in cores if c != core)
            tok[k] = {"R": (sl, total[sl]), "W": (sa, total[sa])}
    wait("g", list(total.items()))
